import numpy as np
import ml_dtypes


def mxq(x, axis, fmt="e4m3"):
    dtype, down = {"e4m3": (ml_dtypes.float8_e4m3fn, 7), "e5m2": (ml_dtypes.float8_e5m2, 14)}[fmt]
    v = np.moveaxis(np.asarray(x, np.float32).astype(ml_dtypes.bfloat16).astype(np.float64), axis, -1)
    blocks = v.reshape(v.shape[:-1] + (-1, 32))
    amax = np.abs(blocks).max(-1, keepdims=True)
    byte = np.maximum(np.where(amax > 0, np.frexp(amax)[1] - 1 + 127, 0) - down, 1)
    scale = np.exp2(byte - 127.0)
    codes = (blocks / scale).astype(np.float32).astype(dtype).astype(np.float64)
    return np.moveaxis((codes * scale).reshape(v.shape), -1, axis)


WIDE = False


def mx_kscale(k):
    if not WIDE:
        return np.ones(k)
    levels = np.array([10, -10, 5, -5, 0])
    if k % 512:
        return np.exp2(np.random.permutation(np.resize(levels, k // 32))).repeat(32)
    a = np.empty((k // 512, 16))
    for p in range(k // 512):
        a[p, :8] = np.random.permutation(np.resize(levels, 8))
        for g in range(8):
            far = levels[np.abs(levels - a[p, g]) >= 10]
            a[p, g + 8] = far[np.random.randint(len(far))]
    return np.exp2(a.ravel()).repeat(32)


def f64(x):
    return np.asarray(x).astype(np.float64)


def striped(idx):
    return np.tile(idx.reshape(-1, 16).T, (8, 1)).astype(np.uint16)


def unstriped(offs):
    return offs[:16].T.reshape(-1).astype(np.int64)


def pack_weight(w):
    k, n = w.shape
    w = f64(np.asarray(w, np.float32).astype(ml_dtypes.bfloat16)).reshape(k // 32, 32, n)
    amax = np.abs(w).max(1)
    byte = np.clip(np.where(amax > 0, np.frexp(amax)[1] - 1 + 127 - 7, 1), 1, 254)
    scaled = (w * np.exp2(127.0 - byte)[:, None, :]).reshape(k, n).astype(np.float32)
    words = np.ascontiguousarray(scaled.reshape(k // 512, 128, 4, n).transpose(0, 1, 3, 2)).astype(ml_dtypes.float8_e4m3fn).view(np.uint8)
    return words, np.ascontiguousarray(byte.astype(np.uint8).reshape(k // 512, 16, n))


def unpack_weight(words, scales):
    g, p, n, _ = words.shape
    vals = np.ascontiguousarray(words).view(ml_dtypes.float8_e4m3fn).astype(np.float64) * np.repeat(np.exp2(scales.astype(np.float64) - 127.0), 8, axis=1)[..., None]
    return vals.transpose(0, 1, 3, 2).reshape(g * 512, n)


E2M1 = np.array([0.0, 0.5, 1.0, 1.5, 2.0, 3.0, 4.0, 6.0, -0.0, -0.5, -1.0, -1.5, -2.0, -3.0, -4.0, -6.0])


def pack_fp4(w):
    k, n = w.shape
    w = f64(np.asarray(w, np.float32).astype(ml_dtypes.bfloat16)).reshape(k // 32, 32, n)
    amax = np.abs(w).max(1)
    mant, ex = np.frexp(amax / 6.0)
    byte = np.clip(np.where(amax > 0, np.where(mant > 0.5, ex, ex - 1) + 127, 1), 1, 254)
    scaled = (w * np.exp2(127.0 - byte)[:, None, :]).reshape(k, n).astype(np.float32)
    c = np.ascontiguousarray(scaled.reshape(k // 512, 128, 4, n).transpose(0, 1, 3, 2)).astype(ml_dtypes.float4_e2m1fn).view(np.uint8) & 0xF
    words = (c[..., 0::2] | (c[..., 1::2] << 4)).reshape(k // 512, 128, 2 * n)
    return np.ascontiguousarray(words), np.ascontiguousarray(byte.astype(np.uint8).reshape(k // 512, 16, n))


def unpack_fp4(words, scales):
    g, _, n = scales.shape
    words = np.ascontiguousarray(words).reshape(g, 128, n, 2)
    nib = np.empty((g, 128, n, 4), np.uint8)
    nib[..., 0::2] = words & 0xF
    nib[..., 1::2] = words >> 4
    vals = E2M1[nib] * np.repeat(np.exp2(scales.astype(np.float64) - 127.0), 8, axis=1)[..., None]
    return vals.transpose(0, 1, 3, 2).reshape(g * 512, n)


def relu(v):
    return np.maximum(v, 0.0)


K, T, S, V, H, N = 512, 2048, 1536, 512, 512, 256


def setup_inputs():
    n = np.random.standard_normal
    s = mx_kscale(K)[:, None]
    u = mx_kscale(H)
    packed_xT = pack_weight(n((K, T)) * s)
    packed_w4 = pack_fp4(n((H, N)) / np.sqrt(H) / u[:, None])
    return {
        "x_words": packed_xT[0],
        "x_scales": packed_xT[1],
        "w1": (n((K, H)) / np.sqrt(K) / s * u).astype(np.float32),
        "w2": (n((K, H)) / np.sqrt(K) / s).astype(np.float32),
        "w3": (n((K, H)) / np.sqrt(K) / s).astype(np.float32),
        "w4_words": packed_w4[0],
        "w4_scales": packed_w4[1],
        "offs": striped(np.random.permutation(T)[:S]),
    }


def reference(x_words, x_scales, w1, w2, w3, w4_words, w4_scales, offs):
    xq = unpack_weight(x_words, x_scales)[:, unstriped(offs)]
    z = (((mxq(f64(w1), 0, "e4m3").T @ xq[:, :V])) * ((mxq(f64(w2), 0, "e4m3").T @ xq[:, V:2 * V]))) * ((mxq(f64(w3), 0, "e4m3").T @ xq[:, 2 * V:3 * V]))
    return relu(unpack_fp4(w4_words, w4_scales).T @ mxq(z, 0, "e4m3"))

@@ -1,0 +1,158 @@
+from contextlib import ExitStack
+
+import concourse.mybir as mybir
+
+K, T, S, V, H, N = 512, 2048, 1536, 512, 512, 256
+FLOPS = 2 * K * H * V * 3 + 2 * H * N * V
+
+F32 = mybir.dt.float32
+BF16 = mybir.dt.bfloat16
+I32 = mybir.dt.int32
+U32 = mybir.dt.uint32
+U16 = mybir.dt.uint16
+U8 = mybir.dt.uint8
+FP8X4 = mybir.dt.float8_e4m3fn_x4
+FP4X4 = mybir.dt.float4_e2m1fn_x4
+MULT = mybir.AluOpType.mult
+RELU = mybir.ActivationFunctionType.Relu
+
+P = 128
+PACK = 4
+CH = 128
+NCH = V // CH
+W3_SCALAR = 88
+
+
+def tile_picked_trilin_relu_p_kernel(tc, x_words, x_scales, w1, w2, w3, w4_words, w4_scales, offs, out):
+    nc = tc.nc
+    with ExitStack() as ctx:
+        keep = ctx.enter_context(tc.tile_pool(name="keep", bufs=1))
+        psum = ctx.enter_context(tc.psum_pool(name="psum", bufs=1))
+
+        offsets = keep.tile([P, S // 16], U16, name="offsets")
+        nc.sync.dma_start(offsets[:], offs)
+
+        def load_scales(name, src, width):
+            plane = keep.tile([P, width], U8, name=name, align_bytes=64)
+            nc.vector.memset(plane[:].bitcast(I32), 0)
+            rows = src[0].bitcast(I32).rearrange("(q r) c -> r q c", r=4)
+            for r in range(4):
+                nc.sync.dma_start(plane[r:P:32, :].bitcast(I32), rows[r])
+            return plane
+
+        def load_weight(name, w, c0, c1):
+            raw = keep.tile([P, PACK, c1 - c0], F32, name=name, align_bytes=64)
+            nc.sync.dma_start(raw[:], w.rearrange("(p j) c -> p j c", j=PACK)[:, :, c0:c1])
+            return raw
+
+        x_table = keep.tile([P, T], U32, name="x_table", align_bytes=64)
+        nc.sync.dma_start(x_table[:].bitcast(I32), x_words[0].rearrange("p c r -> p (c r)").bitcast(I32))
+        raw1 = [load_weight("raw1_%d" % h, w1, h * H // 2, (h + 1) * H // 2) for h in range(2)]
+        x_plane = load_scales("x_plane", x_scales, T)
+        raw2 = [load_weight("raw2_%d" % h, w2, h * H // 2, (h + 1) * H // 2) for h in range(2)]
+        raw3 = load_weight("raw3", w3, 0, H)
+        w4_codes = keep.tile([P, 2 * N], U8, name="w4_codes", align_bytes=64)
+        nc.sync.dma_start(w4_codes[:].bitcast(I32), w4_words[0].bitcast(I32))
+        w4_plane = load_scales("w4_plane", w4_scales, N)
+
+        grouped = [keep.tile([P, PACK, P, PACK], BF16, name="grouped%d" % d, align_bytes=64) for d in range(3)]
+        w_codes = [keep.tile([P, H], U32, name="w_codes%d" % d, align_bytes=64) for d in range(3)]
+        w_plane = [keep.tile([P, H], U8, name="w_plane%d" % d, align_bytes=64) for d in range(3)]
+        picked = [keep.tile([P, V], U32, name="picked%d" % d, align_bytes=64) for d in range(3)]
+        picked_plane = []
+
+        def cast(copy, d, raw, raw_m0, m0, m1):
+            src = raw[:].rearrange("p j (m t) -> p m j t", t=PACK)[:, m0 - raw_m0 : m1 - raw_m0]
+            dst = grouped[d][:].rearrange("p t m j -> p m j t")[:, m0:m1]
+            copy(out=dst, in_=src)
+
+        def quantize_weight(d):
+            nc.vector.quantize_mx(
+                out=w_codes[d][:].bitcast(FP8X4),
+                scales=w_plane[d][:],
+                in_=grouped[d][:].rearrange("p t m j -> p (t m j)"),
+            )
+
+        def gather_words(d):
+            piece = offsets[:, d * V // 16 : (d + 1) * V // 16]
+            nc.vector.tensor_copy(picked[d][:], x_table[:].indirect(piece))
+
+        def gather_scales(d, tag):
+            piece = offsets[:, d * V // 16 : (d + 1) * V // 16]
+            plane = keep.tile([P, V], U8, name="picked_plane%d" % d, tag=tag, align_bytes=64)
+            nc.vector.tensor_copy(plane[:], x_plane[:].indirect(piece))
+            picked_plane.append(plane)
+
+        def product(d, c, tag):
+            bank = psum.tile([P, PACK, CH], F32, name="bank", tag=tag)
+            for t in range(PACK):
+                nc.tensor.matmul_mx(
+                    out=bank[:, t, :],
+                    lhsT=w_codes[d][:, t * P : (t + 1) * P].bitcast(FP8X4),
+                    lhsT_scale=w_plane[d][:, t * P : (t + 1) * P],
+                    rhs=picked[d][:, c * CH : (c + 1) * CH].bitcast(FP8X4),
+                    rhs_scale=picked_plane[d][:, c * CH : (c + 1) * CH],
+                    start=True,
+                    stop=True,
+                )
+            return bank[:].rearrange("p t v -> p v t")
+
+        for d in range(3):
+            gather_words(d)
+        for h in range(2):
+            cast(nc.scalar.copy, 0, raw1[h], h * P // 2, h * P // 2, (h + 1) * P // 2)
+        gather_scales(0, "picked_plane0")
+        quantize_weight(0)
+        gather_scales(1, "raw1_1")
+        for h in range(2):
+            cast(nc.scalar.copy, 1, raw2[h], h * P // 2, h * P // 2, (h + 1) * P // 2)
+        quantize_weight(1)
+        gather_scales(2, "raw2_1")
+
+        first = []
+        for c in range(NCH):
+            a = keep.tile([P, CH, PACK], F32, name="first%d" % c, align_bytes=64)
+            nc.scalar.copy(out=a[:], in_=product(0, c, "lo%d" % c))
+            first.append(a)
+        cast(nc.scalar.copy, 2, raw3, 0, 0, W3_SCALAR)
+        pair = []
+
+        def multiply_pair(c, tag):
+            ab = keep.tile([P, CH, PACK], F32, name="pair%d" % c, tag=tag, align_bytes=64)
+            nc.vector.tensor_tensor(ab[:], product(1, c, "hi%d" % c), first[c][:], MULT)
+            pair.append(ab)
+
+        for c in range(NCH - 1):
+            multiply_pair(c, "pair%d" % c)
+        cast(nc.vector.tensor_copy, 2, raw3, 0, W3_SCALAR, P)
+        quantize_weight(2)
+        multiply_pair(NCH - 1, "raw3")
+
+        out_v = out.rearrange("(u p) v -> p u v", p=P)
+        z = []
+        for c in range(NCH + 1):
+            if c < NCH:
+                zc = keep.tile([P, CH, PACK], BF16, name="z%d" % c, align_bytes=64)
+                nc.vector.tensor_tensor(zc[:], product(2, c, "lo%d" % c), pair[c][:], MULT)
+                z.append(zc)
+            if c > 0:
+                e = c - 1
+                z_codes = keep.tile([P, CH], U32, name="z_codes%d" % e, align_bytes=64)
+                z_plane = keep.tile([P, CH], U8, name="z_plane%d" % e, align_bytes=64)
+                nc.vector.quantize_mx(
+                    out=z_codes[:].bitcast(FP8X4), scales=z_plane[:], in_=z[e][:].rearrange("p v t -> p (v t)")
+                )
+                bank = psum.tile([P, PACK, CH], F32, name="bank", tag="hi%d" % e)
+                for u in range(N // P):
+                    nc.tensor.matmul_mx(
+                        out=bank[:, u, :],
+                        lhsT=w4_codes[:, 2 * u * P : 2 * (u + 1) * P].bitcast(FP4X4),
+                        lhsT_scale=w4_plane[:, u * P : (u + 1) * P],
+                        rhs=z_codes[:].bitcast(FP8X4),
+                        rhs_scale=z_plane[:],
+                        start=True,
+                        stop=True,
+                    )
+                res = keep.tile([P, N // P, CH], F32, name="res%d" % e, align_bytes=64)
+                nc.scalar.activation(res[:], bank[:, 0 : N // P, :], RELU)
+                nc.sync.dma_start(out_v[:, :, e * CH : (e + 1) * CH], res[:])

@@ -20,7 +20,8 @@ P = 128
 PACK = 4
 CH = 128
 NCH = V // CH
-W3_SCALAR = 88
+W3_SCALAR = 76
+X_HEAD = 512
 
 
 def tile_picked_trilin_relu_p_kernel(tc, x_words, x_scales, w1, w2, w3, w4_words, w4_scales, offs, out):
@@ -46,20 +47,22 @@ def tile_picked_trilin_relu_p_kernel(tc, x_words, x_scales, w1, w2, w3, w4_words
             return raw
 
         x_table = keep.tile([P, T], U32, name="x_table", align_bytes=64)
-        nc.sync.dma_start(x_table[:].bitcast(I32), x_words[0].rearrange("p c r -> p (c r)").bitcast(I32))
-        raw1 = [load_weight("raw1_%d" % h, w1, h * H // 2, (h + 1) * H // 2) for h in range(2)]
+        x_src = x_words[0].rearrange("p c r -> p (c r)").bitcast(I32)
+        nc.sync.dma_start(x_table[:, :X_HEAD].bitcast(I32), x_src[:, :X_HEAD])
         x_plane = load_scales("x_plane", x_scales, T)
+        raw1 = [load_weight("raw1_%d" % h, w1, h * H // 2, (h + 1) * H // 2) for h in range(2)]
+        nc.sync.dma_start(x_table[:, X_HEAD:].bitcast(I32), x_src[:, X_HEAD:])
         raw2 = [load_weight("raw2_%d" % h, w2, h * H // 2, (h + 1) * H // 2) for h in range(2)]
         raw3 = load_weight("raw3", w3, 0, H)
         w4_codes = keep.tile([P, 2 * N], U8, name="w4_codes", align_bytes=64)
         nc.sync.dma_start(w4_codes[:].bitcast(I32), w4_words[0].bitcast(I32))
         w4_plane = load_scales("w4_plane", w4_scales, N)
 
-        grouped = [keep.tile([P, PACK, P, PACK], BF16, name="grouped%d" % d, align_bytes=64) for d in range(3)]
+        grouped = [keep.tile([P, PACK, P, PACK], BF16, name="grouped%d" % d, align_bytes=64) for d in range(2)]
         w_codes = [keep.tile([P, H], U32, name="w_codes%d" % d, align_bytes=64) for d in range(3)]
         w_plane = [keep.tile([P, H], U8, name="w_plane%d" % d, align_bytes=64) for d in range(3)]
-        picked = [keep.tile([P, V], U32, name="picked%d" % d, align_bytes=64) for d in range(3)]
-        picked_plane = []
+        picked = []
+        picked_plane = keep.tile([P, S], U8, name="picked_plane", align_bytes=64)
 
         def cast(copy, d, raw, raw_m0, m0, m1):
             src = raw[:].rearrange("p j (m t) -> p m j t", t=PACK)[:, m0 - raw_m0 : m1 - raw_m0]
@@ -73,15 +76,11 @@ def tile_picked_trilin_relu_p_kernel(tc, x_words, x_scales, w1, w2, w3, w4_words
                 in_=grouped[d][:].rearrange("p t m j -> p (t m j)"),
             )
 
-        def gather_words(d):
+        def gather_words(d, tag):
             piece = offsets[:, d * V // 16 : (d + 1) * V // 16]
-            nc.vector.tensor_copy(picked[d][:], x_table[:].indirect(piece))
-
-        def gather_scales(d, tag):
-            piece = offsets[:, d * V // 16 : (d + 1) * V // 16]
-            plane = keep.tile([P, V], U8, name="picked_plane%d" % d, tag=tag, align_bytes=64)
-            nc.vector.tensor_copy(plane[:], x_plane[:].indirect(piece))
-            picked_plane.append(plane)
+            words = keep.tile([P, V], U32, name="picked%d" % d, tag=tag, align_bytes=64)
+            nc.vector.tensor_copy(words[:], x_table[:].indirect(piece))
+            picked.append(words)
 
         def product(d, c, tag):
             bank = psum.tile([P, PACK, CH], F32, name="bank", tag=tag)
@@ -91,23 +90,23 @@ def tile_picked_trilin_relu_p_kernel(tc, x_words, x_scales, w1, w2, w3, w4_words
                     lhsT=w_codes[d][:, t * P : (t + 1) * P].bitcast(FP8X4),
                     lhsT_scale=w_plane[d][:, t * P : (t + 1) * P],
                     rhs=picked[d][:, c * CH : (c + 1) * CH].bitcast(FP8X4),
-                    rhs_scale=picked_plane[d][:, c * CH : (c + 1) * CH],
+                    rhs_scale=picked_plane[:, d * V + c * CH : d * V + (c + 1) * CH],
                     start=True,
                     stop=True,
                 )
             return bank[:].rearrange("p t v -> p v t")
 
-        for d in range(3):
-            gather_words(d)
+        nc.vector.tensor_copy(picked_plane[:], x_plane[:].indirect(offsets[:]))
         for h in range(2):
             cast(nc.scalar.copy, 0, raw1[h], h * P // 2, h * P // 2, (h + 1) * P // 2)
-        gather_scales(0, "picked_plane0")
         quantize_weight(0)
-        gather_scales(1, "raw1_1")
+        for d in range(3):
+            gather_words(d, "picked%d" % d)
         for h in range(2):
             cast(nc.scalar.copy, 1, raw2[h], h * P // 2, h * P // 2, (h + 1) * P // 2)
         quantize_weight(1)
-        gather_scales(2, "raw2_1")
+        grouped.append(keep.tile([P, PACK, P, PACK], BF16, name="grouped2", tag="raw2_1", align_bytes=64))
+        cast(nc.vector.tensor_copy, 2, raw3, 0, W3_SCALAR, P)
 
         first = []
         for c in range(NCH):
@@ -124,7 +123,6 @@ def tile_picked_trilin_relu_p_kernel(tc, x_words, x_scales, w1, w2, w3, w4_words
 
         for c in range(NCH - 1):
             multiply_pair(c, "pair%d" % c)
-        cast(nc.vector.tensor_copy, 2, raw3, 0, W3_SCALAR, P)
         quantize_weight(2)
         multiply_pair(NCH - 1, "raw3")
 

@@ -20,14 +20,17 @@ P = 128
 PACK = 4
 CH = 128
 NCH = V // CH
-W3_SCALAR = 76
 X_HEAD = 512
+EARLY = 2
+HALF = H // 2
+W3_VECTOR = 72
 
 
 def tile_picked_trilin_relu_p_kernel(tc, x_words, x_scales, w1, w2, w3, w4_words, w4_scales, offs, out):
     nc = tc.nc
     with ExitStack() as ctx:
         keep = ctx.enter_context(tc.tile_pool(name="keep", bufs=1))
+        shared = ctx.enter_context(tc.tile_pool(name="shared", bufs=1))
         psum = ctx.enter_context(tc.psum_pool(name="psum", bufs=1))
 
         offsets = keep.tile([P, S // 16], U16, name="offsets")
@@ -41,19 +44,25 @@ def tile_picked_trilin_relu_p_kernel(tc, x_words, x_scales, w1, w2, w3, w4_words
                 nc.sync.dma_start(plane[r:P:32, :].bitcast(I32), rows[r])
             return plane
 
-        def load_weight(name, w, c0, c1):
-            raw = keep.tile([P, PACK, c1 - c0], F32, name=name, align_bytes=64)
-            nc.sync.dma_start(raw[:], w.rearrange("(p j) c -> p j c", j=PACK)[:, :, c0:c1])
+        def load_columns(raw, w, c0):
+            nc.sync.dma_start(raw[:], w.rearrange("(p j) c -> p j c", j=PACK)[:, :, c0 : c0 + raw.shape[2]])
             return raw
+
+        def raw_tile(name, width):
+            return keep.tile([P, PACK, width], F32, name=name, align_bytes=64)
 
         x_table = keep.tile([P, T], U32, name="x_table", align_bytes=64)
         x_src = x_words[0].rearrange("p c r -> p (c r)").bitcast(I32)
         nc.sync.dma_start(x_table[:, :X_HEAD].bitcast(I32), x_src[:, :X_HEAD])
         x_plane = load_scales("x_plane", x_scales, T)
-        raw1 = [load_weight("raw1_%d" % h, w1, h * H // 2, (h + 1) * H // 2) for h in range(2)]
+        raw1 = [load_columns(raw_tile("raw1_%d" % h, HALF), w1, h * HALF) for h in range(2)]
         nc.sync.dma_start(x_table[:, X_HEAD:].bitcast(I32), x_src[:, X_HEAD:])
-        raw2 = [load_weight("raw2_%d" % h, w2, h * H // 2, (h + 1) * H // 2) for h in range(2)]
-        raw3 = load_weight("raw3", w3, 0, H)
+        raw2_1 = shared.tile([P, PACK, HALF], F32, name="raw2_1", align_bytes=64, offset=2048)
+        raw2 = [load_columns(raw_tile("raw2_0", HALF), w2, 0), load_columns(raw2_1, w2, HALF)]
+        raw3 = [
+            load_columns(raw_tile("raw3_0", PACK * W3_VECTOR), w3, 0),
+            load_columns(raw_tile("raw3_1", H - PACK * W3_VECTOR), w3, PACK * W3_VECTOR),
+        ]
         w4_codes = keep.tile([P, 2 * N], U8, name="w4_codes", align_bytes=64)
         nc.sync.dma_start(w4_codes[:].bitcast(I32), w4_words[0].bitcast(I32))
         w4_plane = load_scales("w4_plane", w4_scales, N)
@@ -61,7 +70,6 @@ def tile_picked_trilin_relu_p_kernel(tc, x_words, x_scales, w1, w2, w3, w4_words
         grouped = [keep.tile([P, PACK, P, PACK], BF16, name="grouped%d" % d, align_bytes=64) for d in range(2)]
         w_codes = [keep.tile([P, H], U32, name="w_codes%d" % d, align_bytes=64) for d in range(3)]
         w_plane = [keep.tile([P, H], U8, name="w_plane%d" % d, align_bytes=64) for d in range(3)]
-        picked = []
         picked_plane = keep.tile([P, S], U8, name="picked_plane", align_bytes=64)
 
         def cast(copy, d, raw, raw_m0, m0, m1):
@@ -69,18 +77,12 @@ def tile_picked_trilin_relu_p_kernel(tc, x_words, x_scales, w1, w2, w3, w4_words
             dst = grouped[d][:].rearrange("p t m j -> p m j t")[:, m0:m1]
             copy(out=dst, in_=src)
 
-        def quantize_weight(d):
+        def quantize_weight(d, t0, t1):
             nc.vector.quantize_mx(
-                out=w_codes[d][:].bitcast(FP8X4),
-                scales=w_plane[d][:],
-                in_=grouped[d][:].rearrange("p t m j -> p (t m j)"),
+                out=w_codes[d][:, t0 * P : t1 * P].bitcast(FP8X4),
+                scales=w_plane[d][:, t0 * P : t1 * P],
+                in_=grouped[d][:, t0:t1].rearrange("p t m j -> p (t m j)"),
             )
-
-        def gather_words(d, tag):
-            piece = offsets[:, d * V // 16 : (d + 1) * V // 16]
-            words = keep.tile([P, V], U32, name="picked%d" % d, tag=tag, align_bytes=64)
-            nc.vector.tensor_copy(words[:], x_table[:].indirect(piece))
-            picked.append(words)
 
         def product(d, c, tag):
             bank = psum.tile([P, PACK, CH], F32, name="bank", tag=tag)
@@ -89,7 +91,7 @@ def tile_picked_trilin_relu_p_kernel(tc, x_words, x_scales, w1, w2, w3, w4_words
                     out=bank[:, t, :],
                     lhsT=w_codes[d][:, t * P : (t + 1) * P].bitcast(FP8X4),
                     lhsT_scale=w_plane[d][:, t * P : (t + 1) * P],
-                    rhs=picked[d][:, c * CH : (c + 1) * CH].bitcast(FP8X4),
+                    rhs=picked[:, d * V + c * CH : d * V + (c + 1) * CH].bitcast(FP8X4),
                     rhs_scale=picked_plane[:, d * V + c * CH : d * V + (c + 1) * CH],
                     start=True,
                     stop=True,
@@ -99,58 +101,70 @@ def tile_picked_trilin_relu_p_kernel(tc, x_words, x_scales, w1, w2, w3, w4_words
         nc.vector.tensor_copy(picked_plane[:], x_plane[:].indirect(offsets[:]))
         for h in range(2):
             cast(nc.scalar.copy, 0, raw1[h], h * P // 2, h * P // 2, (h + 1) * P // 2)
-        quantize_weight(0)
+        quantize_weight(0, 0, PACK)
+        picked = keep.tile([P, S], U32, name="picked", tag="raw1_1", align_bytes=64)
         for d in range(3):
-            gather_words(d, "picked%d" % d)
+            piece = offsets[:, d * V // 16 : (d + 1) * V // 16]
+            nc.vector.tensor_copy(picked[:, d * V : (d + 1) * V], x_table[:].indirect(piece))
         for h in range(2):
             cast(nc.scalar.copy, 1, raw2[h], h * P // 2, h * P // 2, (h + 1) * P // 2)
-        quantize_weight(1)
-        grouped.append(keep.tile([P, PACK, P, PACK], BF16, name="grouped2", tag="raw2_1", align_bytes=64))
-        cast(nc.vector.tensor_copy, 2, raw3, 0, W3_SCALAR, P)
+        quantize_weight(1, 0, PACK // 2)
+        quantize_weight(1, PACK // 2, PACK)
+        grouped.append(shared.tile([P, PACK, P, PACK], BF16, name="grouped2", align_bytes=64, offset=4096))
+        cast(nc.vector.tensor_copy, 2, raw3[0], 0, 0, W3_VECTOR)
 
-        first = []
+        def columns(tile, c):
+            return tile[:, c * CH * PACK : (c + 1) * CH * PACK].rearrange("p (v t) -> p v t", t=PACK)
+
+        first_bank = [product(0, c, "lo%d" % c) for c in range(NCH)]
+        first_head = shared.tile([P, EARLY * CH * PACK], F32, name="first_head", align_bytes=64, offset=0)
+        first = [columns(first_head, c) for c in range(EARLY)]
+        for c in range(EARLY):
+            nc.scalar.copy(out=first[c], in_=first_bank[c])
+        cast(nc.scalar.copy, 2, raw3[1], W3_VECTOR, W3_VECTOR, P)
+        first_tail = keep.tile([P, (NCH - EARLY) * CH * PACK], F32, name="first_tail", tag="raw3_1", align_bytes=64)
+        first.extend(columns(first_tail, c) for c in range(NCH - EARLY))
+        for c in range(EARLY, NCH):
+            nc.scalar.copy(out=first[c], in_=first_bank[c])
+
+        pair_all = keep.tile([P, V * PACK], F32, name="pair", tag="raw3_0", align_bytes=64)
+        pair = [columns(pair_all, c) for c in range(NCH)]
         for c in range(NCH):
-            a = keep.tile([P, CH, PACK], F32, name="first%d" % c, align_bytes=64)
-            nc.scalar.copy(out=a[:], in_=product(0, c, "lo%d" % c))
-            first.append(a)
-        cast(nc.scalar.copy, 2, raw3, 0, 0, W3_SCALAR)
-        pair = []
-
-        def multiply_pair(c, tag):
-            ab = keep.tile([P, CH, PACK], F32, name="pair%d" % c, tag=tag, align_bytes=64)
-            nc.vector.tensor_tensor(ab[:], product(1, c, "hi%d" % c), first[c][:], MULT)
-            pair.append(ab)
-
-        for c in range(NCH - 1):
-            multiply_pair(c, "pair%d" % c)
-        quantize_weight(2)
-        multiply_pair(NCH - 1, "raw3")
+            if c == EARLY:
+                quantize_weight(2, 0, PACK)
+            nc.vector.tensor_tensor(pair[c], product(1, c, "hi%d" % c), first[c], MULT)
 
         out_v = out.rearrange("(u p) v -> p u v", p=P)
         z = []
+
+        def multiply_third(c):
+            zc = keep.tile([P, CH, PACK], BF16, name="z%d" % c, align_bytes=64)
+            nc.vector.tensor_tensor(zc[:], product(2, c, "lo%d" % c), pair[c], MULT)
+            z.append(zc)
+
+        def last_layer(e):
+            z_codes = keep.tile([P, CH], U32, name="z_codes%d" % e, align_bytes=64)
+            z_plane = keep.tile([P, CH], U8, name="z_plane%d" % e, align_bytes=64)
+            nc.vector.quantize_mx(
+                out=z_codes[:].bitcast(FP8X4), scales=z_plane[:], in_=z[e][:].rearrange("p v t -> p (v t)")
+            )
+            bank = psum.tile([P, PACK, CH], F32, name="bank", tag="hi%d" % e)
+            for u in range(N // P):
+                nc.tensor.matmul_mx(
+                    out=bank[:, u, :],
+                    lhsT=w4_codes[:, 2 * u * P : 2 * (u + 1) * P].bitcast(FP4X4),
+                    lhsT_scale=w4_plane[:, u * P : (u + 1) * P],
+                    rhs=z_codes[:].bitcast(FP8X4),
+                    rhs_scale=z_plane[:],
+                    start=True,
+                    stop=True,
+                )
+            res = keep.tile([P, N // P, CH], F32, name="res%d" % e, align_bytes=64)
+            nc.scalar.activation(res[:], bank[:, 0 : N // P, :], RELU)
+            nc.sync.dma_start(out_v[:, :, e * CH : (e + 1) * CH], res[:])
+
         for c in range(NCH + 1):
             if c < NCH:
-                zc = keep.tile([P, CH, PACK], BF16, name="z%d" % c, align_bytes=64)
-                nc.vector.tensor_tensor(zc[:], product(2, c, "lo%d" % c), pair[c][:], MULT)
-                z.append(zc)
+                multiply_third(c)
             if c > 0:
-                e = c - 1
-                z_codes = keep.tile([P, CH], U32, name="z_codes%d" % e, align_bytes=64)
-                z_plane = keep.tile([P, CH], U8, name="z_plane%d" % e, align_bytes=64)
-                nc.vector.quantize_mx(
-                    out=z_codes[:].bitcast(FP8X4), scales=z_plane[:], in_=z[e][:].rearrange("p v t -> p (v t)")
-                )
-                bank = psum.tile([P, PACK, CH], F32, name="bank", tag="hi%d" % e)
-                for u in range(N // P):
-                    nc.tensor.matmul_mx(
-                        out=bank[:, u, :],
-                        lhsT=w4_codes[:, 2 * u * P : 2 * (u + 1) * P].bitcast(FP4X4),
-                        lhsT_scale=w4_plane[:, u * P : (u + 1) * P],
-                        rhs=z_codes[:].bitcast(FP8X4),
-                        rhs_scale=z_plane[:],
-                        start=True,
-                        stop=True,
-                    )
-                res = keep.tile([P, N // P, CH], F32, name="res%d" % e, align_bytes=64)
-                nc.scalar.activation(res[:], bank[:, 0 : N // P, :], RELU)
-                nc.sync.dma_start(out_v[:, :, e * CH : (e + 1) * CH], res[:])
+                last_layer(c - 1)

@@ -14,6 +14,7 @@ U8 = mybir.dt.uint8
 FP8X4 = mybir.dt.float8_e4m3fn_x4
 FP4X4 = mybir.dt.float4_e2m1fn_x4
 MULT = mybir.AluOpType.mult
+ADD = mybir.AluOpType.add
 RELU = mybir.ActivationFunctionType.Relu
 
 P = 128
@@ -23,7 +24,7 @@ NCH = V // CH
 X_HEAD = 512
 EARLY = 2
 HALF = H // 2
-W3_VECTOR = 72
+W2_GPSIMD = 24
 
 
 def tile_picked_trilin_relu_p_kernel(tc, x_words, x_scales, w1, w2, w3, w4_words, w4_scales, offs, out):
@@ -57,12 +58,9 @@ def tile_picked_trilin_relu_p_kernel(tc, x_words, x_scales, w1, w2, w3, w4_words
         x_plane = load_scales("x_plane", x_scales, T)
         raw1 = [load_columns(raw_tile("raw1_%d" % h, HALF), w1, h * HALF) for h in range(2)]
         nc.sync.dma_start(x_table[:, X_HEAD:].bitcast(I32), x_src[:, X_HEAD:])
-        raw2_1 = shared.tile([P, PACK, HALF], F32, name="raw2_1", align_bytes=64, offset=2048)
+        raw2_1 = shared.tile([P, PACK, HALF], F32, name="raw2_1", align_bytes=64, offset=4032)
         raw2 = [load_columns(raw_tile("raw2_0", HALF), w2, 0), load_columns(raw2_1, w2, HALF)]
-        raw3 = [
-            load_columns(raw_tile("raw3_0", PACK * W3_VECTOR), w3, 0),
-            load_columns(raw_tile("raw3_1", H - PACK * W3_VECTOR), w3, PACK * W3_VECTOR),
-        ]
+        raw3 = [load_columns(raw_tile("raw3_%d" % h, HALF), w3, h * HALF) for h in range(2)]
         w4_codes = keep.tile([P, 2 * N], U8, name="w4_codes", align_bytes=64)
         nc.sync.dma_start(w4_codes[:].bitcast(I32), w4_words[0].bitcast(I32))
         w4_plane = load_scales("w4_plane", w4_scales, N)
@@ -76,6 +74,11 @@ def tile_picked_trilin_relu_p_kernel(tc, x_words, x_scales, w1, w2, w3, w4_words
             src = raw[:].rearrange("p j (m t) -> p m j t", t=PACK)[:, m0 - raw_m0 : m1 - raw_m0]
             dst = grouped[d][:].rearrange("p t m j -> p m j t")[:, m0:m1]
             copy(out=dst, in_=src)
+
+        def cast_gpsimd(d, raw, raw_m0, m0, m1):
+            src = raw[:].rearrange("p j (m t) -> p m t j", t=PACK)[:, m0 - raw_m0 : m1 - raw_m0]
+            dst = grouped[d][:].rearrange("p t m j -> p m t j")[:, m0:m1]
+            nc.gpsimd.tensor_scalar(dst, src, 1.0, 0.0, MULT, ADD)
 
         def quantize_weight(d, t0, t1):
             nc.vector.quantize_mx(
@@ -91,7 +94,7 @@ def tile_picked_trilin_relu_p_kernel(tc, x_words, x_scales, w1, w2, w3, w4_words
                     out=bank[:, t, :],
                     lhsT=w_codes[d][:, t * P : (t + 1) * P].bitcast(FP8X4),
                     lhsT_scale=w_plane[d][:, t * P : (t + 1) * P],
-                    rhs=picked[:, d * V + c * CH : d * V + (c + 1) * CH].bitcast(FP8X4),
+                    rhs=where[d * V + c * CH].bitcast(FP8X4),
                     rhs_scale=picked_plane[:, d * V + c * CH : d * V + (c + 1) * CH],
                     start=True,
                     stop=True,
@@ -99,40 +102,54 @@ def tile_picked_trilin_relu_p_kernel(tc, x_words, x_scales, w1, w2, w3, w4_words
             return bank[:].rearrange("p t v -> p v t")
 
         nc.vector.tensor_copy(picked_plane[:], x_plane[:].indirect(offsets[:]))
-        for h in range(2):
-            cast(nc.scalar.copy, 0, raw1[h], h * P // 2, h * P // 2, (h + 1) * P // 2)
+        cast(nc.scalar.copy, 0, raw1[0], 0, 0, P // 2)
+        cast(nc.scalar.copy, 0, raw1[1], P // 2, P // 2, P)
         quantize_weight(0, 0, PACK)
-        picked = keep.tile([P, S], U32, name="picked", tag="raw1_1", align_bytes=64)
-        for d in range(3):
-            piece = offsets[:, d * V // 16 : (d + 1) * V // 16]
-            nc.vector.tensor_copy(picked[:, d * V : (d + 1) * V], x_table[:].indirect(piece))
-        for h in range(2):
-            cast(nc.scalar.copy, 1, raw2[h], h * P // 2, h * P // 2, (h + 1) * P // 2)
-        quantize_weight(1, 0, PACK // 2)
-        quantize_weight(1, PACK // 2, PACK)
-        grouped.append(shared.tile([P, PACK, P, PACK], BF16, name="grouped2", align_bytes=64, offset=4096))
-        cast(nc.vector.tensor_copy, 2, raw3[0], 0, 0, W3_VECTOR)
+        where = {}
+
+        def gather_words(tile, runs):
+            col = 0
+            for e0, e1 in runs:
+                nc.vector.tensor_copy(tile[:, col : col + e1 - e0], x_table[:].indirect(offsets[:, e0 // 16 : e1 // 16]))
+                for e in range(e0, e1, CH):
+                    where[e] = tile[:, col + e - e0 : col + e - e0 + CH]
+                col += e1 - e0
+
+        picked = keep.tile([P, 2 * V], U32, name="picked", tag="raw1_1", align_bytes=64)
+        gather_words(picked, [(0, V // 2), (V, 2 * V), (2 * V, 2 * V + V // 2)])
+        cast(nc.scalar.copy, 1, raw2[0], 0, 0, P // 2)
+        cast_gpsimd(1, raw2[1], P // 2, P - W2_GPSIMD, P)
+        cast(nc.scalar.copy, 1, raw2[1], P // 2, P // 2, P - W2_GPSIMD)
+        quantize_weight(1, 0, PACK)
+        picked_late = shared.tile([P, V], U32, name="picked_late", align_bytes=64, offset=4096)
+        gather_words(picked_late, [(V // 2, V), (S - V // 2, S)])
+        grouped.append(shared.tile([P, PACK, P, PACK], BF16, name="grouped2", align_bytes=64, offset=6144))
+        cast_gpsimd(2, raw3[0], 0, 0, P // 2)
 
         def columns(tile, c):
             return tile[:, c * CH * PACK : (c + 1) * CH * PACK].rearrange("p (v t) -> p v t", t=PACK)
 
-        first_bank = [product(0, c, "lo%d" % c) for c in range(NCH)]
+        first_bank = [product(0, c, "lo%d" % c) for c in range(EARLY)]
+        second_bank = [product(1, c, "hi%d" % c) for c in range(EARLY)]
+        first_bank.extend(product(0, c, "lo%d" % c) for c in range(EARLY, NCH))
+        second_bank.extend(product(1, c, "hi%d" % c) for c in range(EARLY, NCH))
         first_head = shared.tile([P, EARLY * CH * PACK], F32, name="first_head", align_bytes=64, offset=0)
         first = [columns(first_head, c) for c in range(EARLY)]
         for c in range(EARLY):
             nc.scalar.copy(out=first[c], in_=first_bank[c])
-        cast(nc.scalar.copy, 2, raw3[1], W3_VECTOR, W3_VECTOR, P)
+        cast(nc.scalar.copy, 2, raw3[1], P // 2, P // 2, P)
         first_tail = keep.tile([P, (NCH - EARLY) * CH * PACK], F32, name="first_tail", tag="raw3_1", align_bytes=64)
         first.extend(columns(first_tail, c) for c in range(NCH - EARLY))
         for c in range(EARLY, NCH):
             nc.scalar.copy(out=first[c], in_=first_bank[c])
 
-        pair_all = keep.tile([P, V * PACK], F32, name="pair", tag="raw3_0", align_bytes=64)
-        pair = [columns(pair_all, c) for c in range(NCH)]
+        pair_head = keep.tile([P, EARLY * CH * PACK], F32, name="pair_head", align_bytes=64)
+        pair_tail = keep.tile([P, (NCH - EARLY) * CH * PACK], F32, name="pair_tail", tag="raw3_0", align_bytes=64)
+        pair = [columns(pair_head, c) for c in range(EARLY)] + [columns(pair_tail, c) for c in range(NCH - EARLY)]
         for c in range(NCH):
             if c == EARLY:
                 quantize_weight(2, 0, PACK)
-            nc.vector.tensor_tensor(pair[c], product(1, c, "hi%d" % c), first[c], MULT)
+            nc.vector.tensor_tensor(pair[c], second_bank[c], first[c], MULT)
 
         out_v = out.rearrange("(u p) v -> p u v", p=P)
         z = []

@@ -23,8 +23,9 @@ CH = 128
 NCH = V // CH
 X_HEAD = 512
 EARLY = 2
-HALF = H // 2
-W2_GPSIMD = 24
+W1_GPSIMD = 52
+W2_GPSIMD = 52
+W3_GPSIMD = 56
 
 
 def tile_picked_trilin_relu_p_kernel(tc, x_words, x_scales, w1, w2, w3, w4_words, w4_scales, offs, out):
@@ -49,23 +50,19 @@ def tile_picked_trilin_relu_p_kernel(tc, x_words, x_scales, w1, w2, w3, w4_words
             nc.sync.dma_start(raw[:], w.rearrange("(p j) c -> p j c", j=PACK)[:, :, c0 : c0 + raw.shape[2]])
             return raw
 
-        def raw_tile(name, width):
-            return keep.tile([P, PACK, width], F32, name=name, align_bytes=64)
-
         x_table = keep.tile([P, T], U32, name="x_table", align_bytes=64)
         x_src = x_words[0].rearrange("p c r -> p (c r)").bitcast(I32)
         nc.sync.dma_start(x_table[:, :X_HEAD].bitcast(I32), x_src[:, :X_HEAD])
         x_plane = load_scales("x_plane", x_scales, T)
-        raw1 = [load_columns(raw_tile("raw1_%d" % h, HALF), w1, h * HALF) for h in range(2)]
         nc.sync.dma_start(x_table[:, X_HEAD:].bitcast(I32), x_src[:, X_HEAD:])
-        raw2_1 = shared.tile([P, PACK, HALF], F32, name="raw2_1", align_bytes=64, offset=4032)
-        raw2 = [load_columns(raw_tile("raw2_0", HALF), w2, 0), load_columns(raw2_1, w2, HALF)]
-        raw3 = [load_columns(raw_tile("raw3_%d" % h, HALF), w3, h * HALF) for h in range(2)]
+        raw1 = load_columns(keep.tile([P, PACK, H], F32, name="raw1", align_bytes=64), w1, 0)
+        raw2 = load_columns(shared.tile([P, PACK, H], F32, name="raw2", align_bytes=64, offset=0), w2, 0)
+        raw3 = load_columns(shared.tile([P, PACK, H], F32, name="raw3", align_bytes=64, offset=8192), w3, 0)
         w4_codes = keep.tile([P, 2 * N], U8, name="w4_codes", align_bytes=64)
         nc.sync.dma_start(w4_codes[:].bitcast(I32), w4_words[0].bitcast(I32))
         w4_plane = load_scales("w4_plane", w4_scales, N)
 
-        grouped = [keep.tile([P, PACK, P, PACK], BF16, name="grouped%d" % d, align_bytes=64) for d in range(2)]
+        grouped = [keep.tile([P, PACK, P, PACK], BF16, name="grouped%d" % d, align_bytes=64) for d in range(3)]
         w_codes = [keep.tile([P, H], U32, name="w_codes%d" % d, align_bytes=64) for d in range(3)]
         w_plane = [keep.tile([P, H], U8, name="w_plane%d" % d, align_bytes=64) for d in range(3)]
         picked_plane = keep.tile([P, S], U8, name="picked_plane", align_bytes=64)
@@ -102,9 +99,6 @@ def tile_picked_trilin_relu_p_kernel(tc, x_words, x_scales, w1, w2, w3, w4_words
             return bank[:].rearrange("p t v -> p v t")
 
         nc.vector.tensor_copy(picked_plane[:], x_plane[:].indirect(offsets[:]))
-        cast(nc.scalar.copy, 0, raw1[0], 0, 0, P // 2)
-        cast(nc.scalar.copy, 0, raw1[1], P // 2, P // 2, P)
-        quantize_weight(0, 0, PACK)
         where = {}
 
         def gather_words(tile, runs):
@@ -115,16 +109,20 @@ def tile_picked_trilin_relu_p_kernel(tc, x_words, x_scales, w1, w2, w3, w4_words
                     where[e] = tile[:, col + e - e0 : col + e - e0 + CH]
                 col += e1 - e0
 
-        picked = keep.tile([P, 2 * V], U32, name="picked", tag="raw1_1", align_bytes=64)
-        gather_words(picked, [(0, V // 2), (V, 2 * V), (2 * V, 2 * V + V // 2)])
-        cast(nc.scalar.copy, 1, raw2[0], 0, 0, P // 2)
-        cast_gpsimd(1, raw2[1], P // 2, P - W2_GPSIMD, P)
-        cast(nc.scalar.copy, 1, raw2[1], P // 2, P // 2, P - W2_GPSIMD)
-        quantize_weight(1, 0, PACK)
-        picked_late = shared.tile([P, V], U32, name="picked_late", align_bytes=64, offset=4096)
-        gather_words(picked_late, [(V // 2, V), (S - V // 2, S)])
-        grouped.append(shared.tile([P, PACK, P, PACK], BF16, name="grouped2", align_bytes=64, offset=6144))
-        cast_gpsimd(2, raw3[0], 0, 0, P // 2)
+        picked = keep.tile([P, V + V // 2], U32, name="picked", align_bytes=64)
+        gather_words(picked, [(0, V // 2), (V, 2 * V)])
+        cast_gpsimd(0, raw1, 0, 0, W1_GPSIMD)
+        cast(nc.scalar.copy, 0, raw1, 0, W1_GPSIMD, P)
+        quantize_weight(0, 0, PACK)
+        picked_mid = keep.tile([P, V], U32, name="picked_mid", tag="raw1", align_bytes=64)
+        gather_words(picked_mid, [(2 * V, S)])
+        cast_gpsimd(1, raw2, 0, 0, W2_GPSIMD)
+        cast(nc.scalar.copy, 1, raw2, 0, W2_GPSIMD, P)
+        for t in range(PACK):
+            quantize_weight(1, t, t + 1)
+        picked_late = shared.tile([P, V // 2], U32, name="picked_late", align_bytes=64, offset=4096)
+        gather_words(picked_late, [(V // 2, V)])
+        cast_gpsimd(2, raw3, 0, 0, W3_GPSIMD)
 
         def columns(tile, c):
             return tile[:, c * CH * PACK : (c + 1) * CH * PACK].rearrange("p (v t) -> p v t", t=PACK)
@@ -137,14 +135,14 @@ def tile_picked_trilin_relu_p_kernel(tc, x_words, x_scales, w1, w2, w3, w4_words
         first = [columns(first_head, c) for c in range(EARLY)]
         for c in range(EARLY):
             nc.scalar.copy(out=first[c], in_=first_bank[c])
-        cast(nc.scalar.copy, 2, raw3[1], P // 2, P // 2, P)
-        first_tail = keep.tile([P, (NCH - EARLY) * CH * PACK], F32, name="first_tail", tag="raw3_1", align_bytes=64)
+        cast(nc.scalar.copy, 2, raw3, 0, W3_GPSIMD, P)
+        first_tail = shared.tile([P, (NCH - EARLY) * CH * PACK], F32, name="first_tail", align_bytes=64, offset=8192)
         first.extend(columns(first_tail, c) for c in range(NCH - EARLY))
         for c in range(EARLY, NCH):
             nc.scalar.copy(out=first[c], in_=first_bank[c])
 
         pair_head = keep.tile([P, EARLY * CH * PACK], F32, name="pair_head", align_bytes=64)
-        pair_tail = keep.tile([P, (NCH - EARLY) * CH * PACK], F32, name="pair_tail", tag="raw3_0", align_bytes=64)
+        pair_tail = shared.tile([P, (NCH - EARLY) * CH * PACK], F32, name="pair_tail", align_bytes=64, offset=12288)
         pair = [columns(pair_head, c) for c in range(EARLY)] + [columns(pair_tail, c) for c in range(NCH - EARLY)]
         for c in range(NCH):
             if c == EARLY:

@@ -21,11 +21,12 @@ P = 128
 PACK = 4
 CH = 128
 NCH = V // CH
-X_HEAD = 512
+X_HEAD = 768
 EARLY = 2
-W1_GPSIMD = 52
+W1_GPSIMD = 56
 W2_GPSIMD = 52
-W3_GPSIMD = 56
+W3_GPSIMD = 84
+HALF = H // 2
 
 
 def tile_picked_trilin_relu_p_kernel(tc, x_words, x_scales, w1, w2, w3, w4_words, w4_scales, offs, out):
@@ -38,12 +39,12 @@ def tile_picked_trilin_relu_p_kernel(tc, x_words, x_scales, w1, w2, w3, w4_words
         offsets = keep.tile([P, S // 16], U16, name="offsets")
         nc.sync.dma_start(offsets[:], offs)
 
-        def load_scales(name, src, width):
+        def load_scales(name, src, width, queues):
             plane = keep.tile([P, width], U8, name=name, align_bytes=64)
             nc.vector.memset(plane[:].bitcast(I32), 0)
             rows = src[0].bitcast(I32).rearrange("(q r) c -> r q c", r=4)
             for r in range(4):
-                nc.sync.dma_start(plane[r:P:32, :].bitcast(I32), rows[r])
+                queues[r % len(queues)].dma_start(plane[r:P:32, :].bitcast(I32), rows[r])
             return plane
 
         def load_columns(raw, w, c0):
@@ -53,14 +54,17 @@ def tile_picked_trilin_relu_p_kernel(tc, x_words, x_scales, w1, w2, w3, w4_words
         x_table = keep.tile([P, T], U32, name="x_table", align_bytes=64)
         x_src = x_words[0].rearrange("p c r -> p (c r)").bitcast(I32)
         nc.sync.dma_start(x_table[:, :X_HEAD].bitcast(I32), x_src[:, :X_HEAD])
-        x_plane = load_scales("x_plane", x_scales, T)
-        nc.sync.dma_start(x_table[:, X_HEAD:].bitcast(I32), x_src[:, X_HEAD:])
+        x_plane = load_scales("x_plane", x_scales, T, [nc.sync, nc.scalar])
         raw1 = load_columns(keep.tile([P, PACK, H], F32, name="raw1", align_bytes=64), w1, 0)
+        nc.sync.dma_start(x_table[:, X_HEAD:].bitcast(I32), x_src[:, X_HEAD:])
         raw2 = load_columns(shared.tile([P, PACK, H], F32, name="raw2", align_bytes=64, offset=0), w2, 0)
-        raw3 = load_columns(shared.tile([P, PACK, H], F32, name="raw3", align_bytes=64, offset=8192), w3, 0)
+        raw3 = [
+            load_columns(keep.tile([P, PACK, HALF], F32, name="raw3_0", align_bytes=64), w3, 0),
+            load_columns(shared.tile([P, PACK, HALF], F32, name="raw3_1", align_bytes=64, offset=10240), w3, HALF),
+        ]
         w4_codes = keep.tile([P, 2 * N], U8, name="w4_codes", align_bytes=64)
         nc.sync.dma_start(w4_codes[:].bitcast(I32), w4_words[0].bitcast(I32))
-        w4_plane = load_scales("w4_plane", w4_scales, N)
+        w4_plane = load_scales("w4_plane", w4_scales, N, [nc.sync])
 
         grouped = [keep.tile([P, PACK, P, PACK], BF16, name="grouped%d" % d, align_bytes=64) for d in range(3)]
         w_codes = [keep.tile([P, H], U32, name="w_codes%d" % d, align_bytes=64) for d in range(3)]
@@ -109,33 +113,30 @@ def tile_picked_trilin_relu_p_kernel(tc, x_words, x_scales, w1, w2, w3, w4_words
                     where[e] = tile[:, col + e - e0 : col + e - e0 + CH]
                 col += e1 - e0
 
-        picked = keep.tile([P, V + V // 2], U32, name="picked", align_bytes=64)
-        gather_words(picked, [(0, V // 2), (V, 2 * V)])
         cast_gpsimd(0, raw1, 0, 0, W1_GPSIMD)
         cast(nc.scalar.copy, 0, raw1, 0, W1_GPSIMD, P)
         quantize_weight(0, 0, PACK)
-        picked_mid = keep.tile([P, V], U32, name="picked_mid", tag="raw1", align_bytes=64)
-        gather_words(picked_mid, [(2 * V, S)])
+        picked = keep.tile([P, S - V // 2], U32, name="picked", tag="raw1", align_bytes=64)
+        gather_words(picked, [(0, V // 2), (V // 2, V), (V, S - V // 2)])
         cast_gpsimd(1, raw2, 0, 0, W2_GPSIMD)
         cast(nc.scalar.copy, 1, raw2, 0, W2_GPSIMD, P)
-        for t in range(PACK):
-            quantize_weight(1, t, t + 1)
+        quantize_weight(1, 0, PACK // 2)
+        quantize_weight(1, PACK // 2, PACK)
         picked_late = shared.tile([P, V // 2], U32, name="picked_late", align_bytes=64, offset=4096)
-        gather_words(picked_late, [(V // 2, V)])
-        cast_gpsimd(2, raw3, 0, 0, W3_GPSIMD)
+        gather_words(picked_late, [(S - V // 2, S)])
+        cast_gpsimd(2, raw3[0], 0, 0, P // 2)
+        cast_gpsimd(2, raw3[1], P // 2, P // 2, W3_GPSIMD)
 
         def columns(tile, c):
             return tile[:, c * CH * PACK : (c + 1) * CH * PACK].rearrange("p (v t) -> p v t", t=PACK)
 
-        first_bank = [product(0, c, "lo%d" % c) for c in range(EARLY)]
-        second_bank = [product(1, c, "hi%d" % c) for c in range(EARLY)]
-        first_bank.extend(product(0, c, "lo%d" % c) for c in range(EARLY, NCH))
-        second_bank.extend(product(1, c, "hi%d" % c) for c in range(EARLY, NCH))
+        first_bank = [product(0, c, "lo%d" % c) for c in range(NCH)]
+        second_bank = [product(1, c, "hi%d" % c) for c in range(NCH)]
         first_head = shared.tile([P, EARLY * CH * PACK], F32, name="first_head", align_bytes=64, offset=0)
         first = [columns(first_head, c) for c in range(EARLY)]
         for c in range(EARLY):
             nc.scalar.copy(out=first[c], in_=first_bank[c])
-        cast(nc.scalar.copy, 2, raw3, 0, W3_GPSIMD, P)
+        cast(nc.scalar.copy, 2, raw3[1], P // 2, W3_GPSIMD, P)
         first_tail = shared.tile([P, (NCH - EARLY) * CH * PACK], F32, name="first_tail", align_bytes=64, offset=8192)
         first.extend(columns(first_tail, c) for c in range(NCH - EARLY))
         for c in range(EARLY, NCH):
@@ -152,10 +153,11 @@ def tile_picked_trilin_relu_p_kernel(tc, x_words, x_scales, w1, w2, w3, w4_words
         out_v = out.rearrange("(u p) v -> p u v", p=P)
         z = []
 
-        def multiply_third(c):
-            zc = keep.tile([P, CH, PACK], BF16, name="z%d" % c, align_bytes=64)
-            nc.vector.tensor_tensor(zc[:], product(2, c, "lo%d" % c), pair[c], MULT)
-            z.append(zc)
+        z.extend(keep.tile([P, CH, PACK], BF16, name="z%d" % c, align_bytes=64) for c in range(NCH))
+        third_bank = [product(2, c, "lo%d" % c) for c in range(NCH)]
+
+        def multiply_third(c, v0, v1):
+            nc.vector.tensor_tensor(z[c][:, v0:v1], third_bank[c][:, v0:v1], pair[c][:, v0:v1], MULT)
 
         def last_layer(e):
             z_codes = keep.tile([P, CH], U32, name="z_codes%d" % e, align_bytes=64)
@@ -164,9 +166,10 @@ def tile_picked_trilin_relu_p_kernel(tc, x_words, x_scales, w1, w2, w3, w4_words
                 out=z_codes[:].bitcast(FP8X4), scales=z_plane[:], in_=z[e][:].rearrange("p v t -> p (v t)")
             )
             bank = psum.tile([P, PACK, CH], F32, name="bank", tag="hi%d" % e)
+            banks = [bank, bank if e < NCH - 1 else psum.tile([P, PACK, CH], F32, name="bank", tag="lo0")]
             for u in range(N // P):
                 nc.tensor.matmul_mx(
-                    out=bank[:, u, :],
+                    out=banks[u][:, u, :],
                     lhsT=w4_codes[:, 2 * u * P : 2 * (u + 1) * P].bitcast(FP4X4),
                     lhsT_scale=w4_plane[:, u * P : (u + 1) * P],
                     rhs=z_codes[:].bitcast(FP8X4),
@@ -175,11 +178,20 @@ def tile_picked_trilin_relu_p_kernel(tc, x_words, x_scales, w1, w2, w3, w4_words
                     stop=True,
                 )
             res = keep.tile([P, N // P, CH], F32, name="res%d" % e, align_bytes=64)
-            nc.scalar.activation(res[:], bank[:, 0 : N // P, :], RELU)
-            nc.sync.dma_start(out_v[:, :, e * CH : (e + 1) * CH], res[:])
+            if e < NCH - 1:
+                nc.scalar.activation(res[:], bank[:, 0 : N // P, :], RELU)
+                nc.sync.dma_start(out_v[:, :, e * CH : (e + 1) * CH], res[:])
+            else:
+                nc.vector.tensor_scalar_max(res[:, 0, :], banks[0][:, 0, :], 0.0)
+                nc.sync.dma_start(out_v[:, 0, e * CH : (e + 1) * CH], res[:, 0, :])
+                nc.scalar.activation(res[:, 1, :], banks[1][:, 1, :], RELU)
+                nc.sync.dma_start(out_v[:, 1, e * CH : (e + 1) * CH], res[:, 1, :])
 
-        for c in range(NCH + 1):
-            if c < NCH:
-                multiply_third(c)
+        for c in range(NCH - 1):
+            multiply_third(c, 0, CH)
             if c > 0:
                 last_layer(c - 1)
+        multiply_third(NCH - 1, 0, CH // 2)
+        last_layer(NCH - 2)
+        multiply_third(NCH - 1, CH // 2, CH)
+        last_layer(NCH - 1)

@@ -23,10 +23,8 @@ CH = 128
 NCH = V // CH
 X_HEAD = 768
 EARLY = 2
-W1_GPSIMD = 56
 W2_GPSIMD = 52
-W3_GPSIMD = 84
-HALF = H // 2
+W3_GPSIMD = 64
 
 
 def tile_picked_trilin_relu_p_kernel(tc, x_words, x_scales, w1, w2, w3, w4_words, w4_scales, offs, out):
@@ -39,12 +37,12 @@ def tile_picked_trilin_relu_p_kernel(tc, x_words, x_scales, w1, w2, w3, w4_words
         offsets = keep.tile([P, S // 16], U16, name="offsets")
         nc.sync.dma_start(offsets[:], offs)
 
-        def load_scales(name, src, width, queues):
+        def load_scales(name, src, width):
             plane = keep.tile([P, width], U8, name=name, align_bytes=64)
             nc.vector.memset(plane[:].bitcast(I32), 0)
             rows = src[0].bitcast(I32).rearrange("(q r) c -> r q c", r=4)
             for r in range(4):
-                queues[r % len(queues)].dma_start(plane[r:P:32, :].bitcast(I32), rows[r])
+                nc.sync.dma_start(plane[r:P:32, :].bitcast(I32), rows[r])
             return plane
 
         def load_columns(raw, w, c0):
@@ -54,19 +52,16 @@ def tile_picked_trilin_relu_p_kernel(tc, x_words, x_scales, w1, w2, w3, w4_words
         x_table = keep.tile([P, T], U32, name="x_table", align_bytes=64)
         x_src = x_words[0].rearrange("p c r -> p (c r)").bitcast(I32)
         nc.sync.dma_start(x_table[:, :X_HEAD].bitcast(I32), x_src[:, :X_HEAD])
-        x_plane = load_scales("x_plane", x_scales, T, [nc.sync, nc.scalar])
+        x_plane = load_scales("x_plane", x_scales, T)
         raw1 = load_columns(keep.tile([P, PACK, H], F32, name="raw1", align_bytes=64), w1, 0)
         nc.sync.dma_start(x_table[:, X_HEAD:].bitcast(I32), x_src[:, X_HEAD:])
         raw2 = load_columns(shared.tile([P, PACK, H], F32, name="raw2", align_bytes=64, offset=0), w2, 0)
-        raw3 = [
-            load_columns(keep.tile([P, PACK, HALF], F32, name="raw3_0", align_bytes=64), w3, 0),
-            load_columns(shared.tile([P, PACK, HALF], F32, name="raw3_1", align_bytes=64, offset=10240), w3, HALF),
-        ]
+        raw3 = load_columns(shared.tile([P, PACK, H], F32, name="raw3", align_bytes=64, offset=8192), w3, 0)
         w4_codes = keep.tile([P, 2 * N], U8, name="w4_codes", align_bytes=64)
         nc.sync.dma_start(w4_codes[:].bitcast(I32), w4_words[0].bitcast(I32))
-        w4_plane = load_scales("w4_plane", w4_scales, N, [nc.sync])
+        w4_plane = load_scales("w4_plane", w4_scales, N)
 
-        grouped = [keep.tile([P, PACK, P, PACK], BF16, name="grouped%d" % d, align_bytes=64) for d in range(3)]
+        grouped = [keep.tile([P, PACK, P, PACK], BF16, name="grouped", align_bytes=64) for d in range(3)]
         w_codes = [keep.tile([P, H], U32, name="w_codes%d" % d, align_bytes=64) for d in range(3)]
         w_plane = [keep.tile([P, H], U8, name="w_plane%d" % d, align_bytes=64) for d in range(3)]
         picked_plane = keep.tile([P, S], U8, name="picked_plane", align_bytes=64)
@@ -113,19 +108,19 @@ def tile_picked_trilin_relu_p_kernel(tc, x_words, x_scales, w1, w2, w3, w4_words
                     where[e] = tile[:, col + e - e0 : col + e - e0 + CH]
                 col += e1 - e0
 
-        cast_gpsimd(0, raw1, 0, 0, W1_GPSIMD)
-        cast(nc.scalar.copy, 0, raw1, 0, W1_GPSIMD, P)
+        picked_early = keep.tile([P, V // 2], U32, name="picked_early", align_bytes=64)
+        gather_words(picked_early, [(0, V // 2)])
+        cast(nc.scalar.copy, 0, raw1, 0, 0, P)
         quantize_weight(0, 0, PACK)
-        picked = keep.tile([P, S - V // 2], U32, name="picked", tag="raw1", align_bytes=64)
-        gather_words(picked, [(0, V // 2), (V // 2, V), (V, S - V // 2)])
+        picked = keep.tile([P, S - V], U32, name="picked", tag="raw1", align_bytes=64)
+        gather_words(picked, [(V // 2, V), (V, S - V // 2)])
         cast_gpsimd(1, raw2, 0, 0, W2_GPSIMD)
         cast(nc.scalar.copy, 1, raw2, 0, W2_GPSIMD, P)
         quantize_weight(1, 0, PACK // 2)
         quantize_weight(1, PACK // 2, PACK)
         picked_late = shared.tile([P, V // 2], U32, name="picked_late", align_bytes=64, offset=4096)
         gather_words(picked_late, [(S - V // 2, S)])
-        cast_gpsimd(2, raw3[0], 0, 0, P // 2)
-        cast_gpsimd(2, raw3[1], P // 2, P // 2, W3_GPSIMD)
+        cast_gpsimd(2, raw3, 0, 0, W3_GPSIMD)
 
         def columns(tile, c):
             return tile[:, c * CH * PACK : (c + 1) * CH * PACK].rearrange("p (v t) -> p v t", t=PACK)
@@ -136,7 +131,7 @@ def tile_picked_trilin_relu_p_kernel(tc, x_words, x_scales, w1, w2, w3, w4_words
         first = [columns(first_head, c) for c in range(EARLY)]
         for c in range(EARLY):
             nc.scalar.copy(out=first[c], in_=first_bank[c])
-        cast(nc.scalar.copy, 2, raw3[1], P // 2, W3_GPSIMD, P)
+        cast(nc.scalar.copy, 2, raw3, 0, W3_GPSIMD, P)
         first_tail = shared.tile([P, (NCH - EARLY) * CH * PACK], F32, name="first_tail", align_bytes=64, offset=8192)
         first.extend(columns(first_tail, c) for c in range(NCH - EARLY))
         for c in range(EARLY, NCH):

@@ -23,8 +23,8 @@ CH = 128
 NCH = V // CH
 X_HEAD = 768
 EARLY = 2
-W2_GPSIMD = 52
-W3_GPSIMD = 64
+W2_VECTOR = 80
+W3_GPSIMD = 50
 
 
 def tile_picked_trilin_relu_p_kernel(tc, x_words, x_scales, w1, w2, w3, w4_words, w4_scales, offs, out):
@@ -71,6 +71,11 @@ def tile_picked_trilin_relu_p_kernel(tc, x_words, x_scales, w1, w2, w3, w4_words
             dst = grouped[d][:].rearrange("p t m j -> p m j t")[:, m0:m1]
             copy(out=dst, in_=src)
 
+        def cast_vector(d, raw, m1, t0, t1):
+            src = raw[:].rearrange("p j (m t) -> p m j t", t=PACK)[:, :m1, :, t0:t1]
+            dst = grouped[d][:].rearrange("p t m j -> p m j t")[:, :m1, :, t0:t1]
+            nc.vector.tensor_copy(out=dst, in_=src)
+
         def cast_gpsimd(d, raw, raw_m0, m0, m1):
             src = raw[:].rearrange("p j (m t) -> p m t j", t=PACK)[:, m0 - raw_m0 : m1 - raw_m0]
             dst = grouped[d][:].rearrange("p t m j -> p m t j")[:, m0:m1]
@@ -112,14 +117,15 @@ def tile_picked_trilin_relu_p_kernel(tc, x_words, x_scales, w1, w2, w3, w4_words
         gather_words(picked_early, [(0, V // 2)])
         cast(nc.scalar.copy, 0, raw1, 0, 0, P)
         quantize_weight(0, 0, PACK)
-        picked = keep.tile([P, S - V], U32, name="picked", tag="raw1", align_bytes=64)
-        gather_words(picked, [(V // 2, V), (V, S - V // 2)])
-        cast_gpsimd(1, raw2, 0, 0, W2_GPSIMD)
-        cast(nc.scalar.copy, 1, raw2, 0, W2_GPSIMD, P)
+        picked = keep.tile([P, V], U32, name="picked", tag="raw1", align_bytes=64)
+        gather_words(picked, [(V // 2, V), (V, V + V // 2)])
+        cast_vector(1, raw2, W2_VECTOR, 0, PACK // 2)
+        cast_vector(1, raw2, W2_VECTOR, PACK // 2, PACK)
+        cast(nc.scalar.copy, 1, raw2, 0, W2_VECTOR, P)
         quantize_weight(1, 0, PACK // 2)
         quantize_weight(1, PACK // 2, PACK)
-        picked_late = shared.tile([P, V // 2], U32, name="picked_late", align_bytes=64, offset=4096)
-        gather_words(picked_late, [(S - V // 2, S)])
+        picked_late = shared.tile([P, V + V // 2], U32, name="picked_late", align_bytes=64, offset=4096)
+        gather_words(picked_late, [(V + V // 2, 2 * V), (2 * V, S)])
         cast_gpsimd(2, raw3, 0, 0, W3_GPSIMD)
 
         def columns(tile, c):
@@ -136,14 +142,19 @@ def tile_picked_trilin_relu_p_kernel(tc, x_words, x_scales, w1, w2, w3, w4_words
         first.extend(columns(first_tail, c) for c in range(NCH - EARLY))
         for c in range(EARLY, NCH):
             nc.scalar.copy(out=first[c], in_=first_bank[c])
+        second_last = shared.tile([P, CH * PACK], F32, name="second_last", align_bytes=64, offset=12288)
+        nc.scalar.copy(out=columns(second_last, 0), in_=second_bank[NCH - 1])
 
-        pair_head = keep.tile([P, EARLY * CH * PACK], F32, name="pair_head", align_bytes=64)
-        pair_tail = shared.tile([P, (NCH - EARLY) * CH * PACK], F32, name="pair_tail", align_bytes=64, offset=12288)
-        pair = [columns(pair_head, c) for c in range(EARLY)] + [columns(pair_tail, c) for c in range(NCH - EARLY)]
-        for c in range(NCH):
-            if c == EARLY:
+        pair_head = keep.tile([P, CH * PACK], F32, name="pair_head", align_bytes=64)
+        pair_tail = shared.tile([P, (NCH - 2) * CH * PACK], F32, name="pair_tail", align_bytes=64, offset=14336)
+        pair = [columns(pair_head, 0)] + [columns(pair_tail, c) for c in range(NCH - 2)]
+        for c in range(NCH - 1):
+            if c == 1:
                 quantize_weight(2, 0, PACK)
             nc.vector.tensor_tensor(pair[c], second_bank[c], first[c], MULT)
+        pair_last = keep.tile([P, CH * PACK], F32, name="pair_last", tag="grouped", align_bytes=64)
+        nc.gpsimd.tensor_tensor(pair_last[:], second_last[:], first_tail[:, CH * PACK :], MULT)
+        pair.append(columns(pair_last, 0))
 
         out_v = out.rearrange("(u p) v -> p u v", p=P)
         z = []
@@ -184,8 +195,8 @@ def tile_picked_trilin_relu_p_kernel(tc, x_words, x_scales, w1, w2, w3, w4_words
 
         for c in range(NCH - 1):
             multiply_third(c, 0, CH)
-            if c > 0:
-                last_layer(c - 1)
+        for c in range(NCH - 2):
+            last_layer(c)
         multiply_third(NCH - 1, 0, CH // 2)
         last_layer(NCH - 2)
         multiply_third(NCH - 1, CH // 2, CH)

@@ -22,9 +22,10 @@ PACK = 4
 CH = 128
 NCH = V // CH
 X_HEAD = 768
-EARLY = 2
-W2_VECTOR = 80
-W3_GPSIMD = 50
+HALF = P // 2
+W1_GPSIMD = 40
+W2_GPSIMD = (24, 24)
+W3_GPSIMD = (32, 22)
 
 
 def tile_picked_trilin_relu_p_kernel(tc, x_words, x_scales, w1, w2, w3, w4_words, w4_scales, offs, out):
@@ -55,8 +56,14 @@ def tile_picked_trilin_relu_p_kernel(tc, x_words, x_scales, w1, w2, w3, w4_words
         x_plane = load_scales("x_plane", x_scales, T)
         raw1 = load_columns(keep.tile([P, PACK, H], F32, name="raw1", align_bytes=64), w1, 0)
         nc.sync.dma_start(x_table[:, X_HEAD:].bitcast(I32), x_src[:, X_HEAD:])
-        raw2 = load_columns(shared.tile([P, PACK, H], F32, name="raw2", align_bytes=64, offset=0), w2, 0)
-        raw3 = load_columns(shared.tile([P, PACK, H], F32, name="raw3", align_bytes=64, offset=8192), w3, 0)
+        raw2 = [
+            load_columns(shared.tile([P, PACK, H // 2], F32, name="raw2%d" % h, align_bytes=64, offset=8192 * h), w2, h * H // 2)
+            for h in range(2)
+        ]
+        raw3 = [
+            load_columns(shared.tile([P, PACK, H // 2], F32, name="raw3%d" % h, align_bytes=64, offset=12288 + 4096 * h), w3, h * H // 2)
+            for h in range(2)
+        ]
         w4_codes = keep.tile([P, 2 * N], U8, name="w4_codes", align_bytes=64)
         nc.sync.dma_start(w4_codes[:].bitcast(I32), w4_words[0].bitcast(I32))
         w4_plane = load_scales("w4_plane", w4_scales, N)
@@ -66,20 +73,14 @@ def tile_picked_trilin_relu_p_kernel(tc, x_words, x_scales, w1, w2, w3, w4_words
         w_plane = [keep.tile([P, H], U8, name="w_plane%d" % d, align_bytes=64) for d in range(3)]
         picked_plane = keep.tile([P, S], U8, name="picked_plane", align_bytes=64)
 
-        def cast(copy, d, raw, raw_m0, m0, m1):
-            src = raw[:].rearrange("p j (m t) -> p m j t", t=PACK)[:, m0 - raw_m0 : m1 - raw_m0]
-            dst = grouped[d][:].rearrange("p t m j -> p m j t")[:, m0:m1]
-            copy(out=dst, in_=src)
-
-        def cast_vector(d, raw, m1, t0, t1):
-            src = raw[:].rearrange("p j (m t) -> p m j t", t=PACK)[:, :m1, :, t0:t1]
-            dst = grouped[d][:].rearrange("p t m j -> p m j t")[:, :m1, :, t0:t1]
-            nc.vector.tensor_copy(out=dst, in_=src)
-
-        def cast_gpsimd(d, raw, raw_m0, m0, m1):
-            src = raw[:].rearrange("p j (m t) -> p m t j", t=PACK)[:, m0 - raw_m0 : m1 - raw_m0]
-            dst = grouped[d][:].rearrange("p t m j -> p m t j")[:, m0:m1]
+        def cast(d, raw, m0, split):
+            groups = raw.shape[2] // PACK
+            src = raw[:].rearrange("p j (m t) -> p m t j", t=PACK)[:, :split]
+            dst = grouped[d][:].rearrange("p t m j -> p m t j")[:, m0 : m0 + split]
             nc.gpsimd.tensor_scalar(dst, src, 1.0, 0.0, MULT, ADD)
+            src = raw[:].rearrange("p j (m t) -> p m j t", t=PACK)[:, split:]
+            dst = grouped[d][:].rearrange("p t m j -> p m j t")[:, m0 + split : m0 + groups]
+            nc.scalar.copy(out=dst, in_=src)
 
         def quantize_weight(d, t0, t1):
             nc.vector.quantize_mx(
@@ -113,47 +114,43 @@ def tile_picked_trilin_relu_p_kernel(tc, x_words, x_scales, w1, w2, w3, w4_words
                     where[e] = tile[:, col + e - e0 : col + e - e0 + CH]
                 col += e1 - e0
 
-        picked_early = keep.tile([P, V // 2], U32, name="picked_early", align_bytes=64)
-        gather_words(picked_early, [(0, V // 2)])
-        cast(nc.scalar.copy, 0, raw1, 0, 0, P)
-        quantize_weight(0, 0, PACK)
-        picked = keep.tile([P, V], U32, name="picked", tag="raw1", align_bytes=64)
-        gather_words(picked, [(V // 2, V), (V, V + V // 2)])
-        cast_vector(1, raw2, W2_VECTOR, 0, PACK // 2)
-        cast_vector(1, raw2, W2_VECTOR, PACK // 2, PACK)
-        cast(nc.scalar.copy, 1, raw2, 0, W2_VECTOR, P)
-        quantize_weight(1, 0, PACK // 2)
-        quantize_weight(1, PACK // 2, PACK)
-        picked_late = shared.tile([P, V + V // 2], U32, name="picked_late", align_bytes=64, offset=4096)
-        gather_words(picked_late, [(V + V // 2, 2 * V), (2 * V, S)])
-        cast_gpsimd(2, raw3, 0, 0, W3_GPSIMD)
-
         def columns(tile, c):
             return tile[:, c * CH * PACK : (c + 1) * CH * PACK].rearrange("p (v t) -> p v t", t=PACK)
 
+        picked_early = keep.tile([P, V // 2], U32, name="picked_early", align_bytes=64)
+        gather_words(picked_early, [(0, V // 2)])
+        cast(0, raw1, 0, W1_GPSIMD)
+        quantize_weight(0, 0, PACK)
+        picked = keep.tile([P, V + V // 2], U32, name="picked", tag="raw1", align_bytes=64)
+        gather_words(picked, [(V // 2, 2 * V)])
         first_bank = [product(0, c, "lo%d" % c) for c in range(NCH)]
+        for h in range(2):
+            cast(1, raw2[h], h * HALF, W2_GPSIMD[h])
+        head = shared.tile([P, 2 * CH * PACK], F32, name="head", align_bytes=64, offset=6144)
+        first = [columns(head, c) for c in range(2)]
+        for c in range(2):
+            nc.scalar.copy(out=first[c], in_=first_bank[c])
+        quantize_weight(1, 0, PACK)
+        picked_late = shared.tile([P, V], U32, name="picked_late", align_bytes=64, offset=10240)
+        gather_words(picked_late, [(2 * V, S)])
         second_bank = [product(1, c, "hi%d" % c) for c in range(NCH)]
-        first_head = shared.tile([P, EARLY * CH * PACK], F32, name="first_head", align_bytes=64, offset=0)
-        first = [columns(first_head, c) for c in range(EARLY)]
-        for c in range(EARLY):
-            nc.scalar.copy(out=first[c], in_=first_bank[c])
-        cast(nc.scalar.copy, 2, raw3, 0, W3_GPSIMD, P)
-        first_tail = shared.tile([P, (NCH - EARLY) * CH * PACK], F32, name="first_tail", align_bytes=64, offset=8192)
-        first.extend(columns(first_tail, c) for c in range(NCH - EARLY))
-        for c in range(EARLY, NCH):
-            nc.scalar.copy(out=first[c], in_=first_bank[c])
-        second_last = shared.tile([P, CH * PACK], F32, name="second_last", align_bytes=64, offset=12288)
-        nc.scalar.copy(out=columns(second_last, 0), in_=second_bank[NCH - 1])
+        for h in range(2):
+            cast(2, raw3[h], h * HALF, W3_GPSIMD[h])
+        tail = shared.tile([P, 3 * CH * PACK], F32, name="tail", align_bytes=64, offset=12288)
+        first.append(columns(tail, 0))
+        nc.scalar.copy(out=columns(tail, 0), in_=first_bank[NCH - 2])
+        nc.scalar.copy(out=columns(tail, 1), in_=first_bank[NCH - 1])
+        nc.scalar.copy(out=columns(tail, 2), in_=second_bank[NCH - 1])
 
         pair_head = keep.tile([P, CH * PACK], F32, name="pair_head", align_bytes=64)
-        pair_tail = shared.tile([P, (NCH - 2) * CH * PACK], F32, name="pair_tail", align_bytes=64, offset=14336)
+        pair_tail = shared.tile([P, (NCH - 2) * CH * PACK], F32, name="pair_tail", align_bytes=64, offset=18432)
         pair = [columns(pair_head, 0)] + [columns(pair_tail, c) for c in range(NCH - 2)]
         for c in range(NCH - 1):
             if c == 1:
                 quantize_weight(2, 0, PACK)
             nc.vector.tensor_tensor(pair[c], second_bank[c], first[c], MULT)
         pair_last = keep.tile([P, CH * PACK], F32, name="pair_last", tag="grouped", align_bytes=64)
-        nc.gpsimd.tensor_tensor(pair_last[:], second_last[:], first_tail[:, CH * PACK :], MULT)
+        nc.gpsimd.tensor_tensor(pair_last[:], tail[:, 2 * CH * PACK :], tail[:, CH * PACK : 2 * CH * PACK], MULT)
         pair.append(columns(pair_last, 0))
 
         out_v = out.rearrange("(u p) v -> p u v", p=P)

@@ -24,8 +24,10 @@ NCH = V // CH
 X_HEAD = 768
 HALF = P // 2
 W1_GPSIMD = 40
-W2_GPSIMD = (24, 24)
-W3_GPSIMD = (32, 22)
+W2_GPSIMD = (16, 24)
+W3_GPSIMD = (30, 22)
+LATE = 384
+SHARE = CH // 2
 
 
 def tile_picked_trilin_relu_p_kernel(tc, x_words, x_scales, w1, w2, w3, w4_words, w4_scales, offs, out):
@@ -75,12 +77,14 @@ def tile_picked_trilin_relu_p_kernel(tc, x_words, x_scales, w1, w2, w3, w4_words
 
         def cast(d, raw, m0, split):
             groups = raw.shape[2] // PACK
-            src = raw[:].rearrange("p j (m t) -> p m t j", t=PACK)[:, :split]
-            dst = grouped[d][:].rearrange("p t m j -> p m t j")[:, m0 : m0 + split]
-            nc.gpsimd.tensor_scalar(dst, src, 1.0, 0.0, MULT, ADD)
-            src = raw[:].rearrange("p j (m t) -> p m j t", t=PACK)[:, split:]
-            dst = grouped[d][:].rearrange("p t m j -> p m j t")[:, m0 + split : m0 + groups]
-            nc.scalar.copy(out=dst, in_=src)
+            if split > 0:
+                src = raw[:].rearrange("p j (m t) -> p m t j", t=PACK)[:, :split]
+                dst = grouped[d][:].rearrange("p t m j -> p m t j")[:, m0 : m0 + split]
+                nc.gpsimd.tensor_scalar(dst, src, 1.0, 0.0, MULT, ADD)
+            if split < groups:
+                src = raw[:].rearrange("p j (m t) -> p m j t", t=PACK)[:, split:]
+                dst = grouped[d][:].rearrange("p t m j -> p m j t")[:, m0 + split : m0 + groups]
+                nc.scalar.copy(out=dst, in_=src)
 
         def quantize_weight(d, t0, t1):
             nc.vector.quantize_mx(
@@ -121,37 +125,50 @@ def tile_picked_trilin_relu_p_kernel(tc, x_words, x_scales, w1, w2, w3, w4_words
         gather_words(picked_early, [(0, V // 2)])
         cast(0, raw1, 0, W1_GPSIMD)
         quantize_weight(0, 0, PACK)
-        picked = keep.tile([P, V + V // 2], U32, name="picked", tag="raw1", align_bytes=64)
-        gather_words(picked, [(V // 2, 2 * V)])
+        picked = keep.tile([P, S - LATE - V // 2], U32, name="picked", tag="raw1", align_bytes=64)
+        gather_words(picked, [(V // 2, V), (V, S - LATE)])
         first_bank = [product(0, c, "lo%d" % c) for c in range(NCH)]
         for h in range(2):
             cast(1, raw2[h], h * HALF, W2_GPSIMD[h])
-        head = shared.tile([P, 2 * CH * PACK], F32, name="head", align_bytes=64, offset=6144)
+        head = shared.tile([P, 2 * CH * PACK], F32, name="head", align_bytes=64, offset=0)
         first = [columns(head, c) for c in range(2)]
         for c in range(2):
             nc.scalar.copy(out=first[c], in_=first_bank[c])
-        quantize_weight(1, 0, PACK)
-        picked_late = shared.tile([P, V], U32, name="picked_late", align_bytes=64, offset=10240)
-        gather_words(picked_late, [(2 * V, S)])
+        quantize_weight(1, 0, PACK // 2)
+        quantize_weight(1, PACK // 2, PACK)
+        picked_late = shared.tile([P, LATE], U32, name="picked_late", align_bytes=64, offset=10240)
+        gather_words(picked_late, [(S - LATE, S)])
         second_bank = [product(1, c, "hi%d" % c) for c in range(NCH)]
         for h in range(2):
             cast(2, raw3[h], h * HALF, W3_GPSIMD[h])
-        tail = shared.tile([P, 3 * CH * PACK], F32, name="tail", align_bytes=64, offset=12288)
-        first.append(columns(tail, 0))
-        nc.scalar.copy(out=columns(tail, 0), in_=first_bank[NCH - 2])
-        nc.scalar.copy(out=columns(tail, 1), in_=first_bank[NCH - 1])
-        nc.scalar.copy(out=columns(tail, 2), in_=second_bank[NCH - 1])
+        first_tail = keep.tile([P, 2 * CH * PACK], F32, name="first_tail", align_bytes=64)
+        second_tail = keep.tile([P, (CH + SHARE) * PACK], F32, name="second_tail", align_bytes=64)
+        first.extend(columns(first_tail, c) for c in range(2))
+        second_view = second_tail[:].rearrange("p (v t) -> p v t", t=PACK)
+        nc.scalar.copy(out=first[2], in_=first_bank[2])
+        nc.scalar.copy(out=second_view[:, :SHARE], in_=second_bank[2][:, CH - SHARE :])
+        nc.scalar.copy(out=first[3], in_=first_bank[3])
+        nc.scalar.copy(out=second_view[:, SHARE:], in_=second_bank[3])
 
         pair_head = keep.tile([P, CH * PACK], F32, name="pair_head", align_bytes=64)
-        pair_tail = shared.tile([P, (NCH - 2) * CH * PACK], F32, name="pair_tail", align_bytes=64, offset=18432)
-        pair = [columns(pair_head, 0)] + [columns(pair_tail, c) for c in range(NCH - 2)]
-        for c in range(NCH - 1):
-            if c == 1:
-                quantize_weight(2, 0, PACK)
-            nc.vector.tensor_tensor(pair[c], second_bank[c], first[c], MULT)
-        pair_last = keep.tile([P, CH * PACK], F32, name="pair_last", tag="grouped", align_bytes=64)
-        nc.gpsimd.tensor_tensor(pair_last[:], tail[:, 2 * CH * PACK :], tail[:, CH * PACK : 2 * CH * PACK], MULT)
-        pair.append(columns(pair_last, 0))
+        pair_tail = shared.tile([P, (2 * CH - SHARE) * PACK], F32, name="pair_tail", align_bytes=64, offset=14336)
+        pair_last = keep.tile([P, (CH + SHARE) * PACK], F32, name="pair_last", tag="grouped", align_bytes=64)
+        tail_view = pair_tail[:].rearrange("p (v t) -> p v t", t=PACK)
+        last_view = pair_last[:].rearrange("p (v t) -> p v t", t=PACK)
+        nc.vector.tensor_tensor(columns(pair_head, 0), second_bank[0], first[0], MULT)
+        quantize_weight(2, 0, PACK // 2)
+        quantize_weight(2, PACK // 2, PACK)
+        nc.vector.tensor_tensor(tail_view[:, :CH], second_bank[1], first[1], MULT)
+        nc.vector.tensor_tensor(tail_view[:, CH:], second_bank[2][:, : CH - SHARE], first[2][:, : CH - SHARE], MULT)
+        cut = SHARE * PACK
+        nc.gpsimd.tensor_tensor(pair_last[:, :cut], second_tail[:, :cut], first_tail[:, CH * PACK - cut : CH * PACK], MULT)
+        nc.gpsimd.tensor_tensor(pair_last[:, cut:], second_tail[:, cut:], first_tail[:, CH * PACK :], MULT)
+        pair = [
+            [(0, CH, columns(pair_head, 0))],
+            [(0, CH, tail_view[:, :CH])],
+            [(0, CH - SHARE, tail_view[:, CH:]), (CH - SHARE, CH, last_view[:, :SHARE])],
+            [(0, CH // 2, last_view[:, SHARE : SHARE + CH // 2]), (CH // 2, CH, last_view[:, SHARE + CH // 2 :])],
+        ]
 
         out_v = out.rearrange("(u p) v -> p u v", p=P)
         z = []
@@ -159,8 +176,9 @@ def tile_picked_trilin_relu_p_kernel(tc, x_words, x_scales, w1, w2, w3, w4_words
         z.extend(keep.tile([P, CH, PACK], BF16, name="z%d" % c, align_bytes=64) for c in range(NCH))
         third_bank = [product(2, c, "lo%d" % c) for c in range(NCH)]
 
-        def multiply_third(c, v0, v1):
-            nc.vector.tensor_tensor(z[c][:, v0:v1], third_bank[c][:, v0:v1], pair[c][:, v0:v1], MULT)
+        def multiply_third(c, part):
+            v0, v1, factor = pair[c][part]
+            nc.vector.tensor_tensor(z[c][:, v0:v1], third_bank[c][:, v0:v1], factor, MULT)
 
         def last_layer(e):
             z_codes = keep.tile([P, CH], U32, name="z_codes%d" % e, align_bytes=64)
@@ -191,10 +209,11 @@ def tile_picked_trilin_relu_p_kernel(tc, x_words, x_scales, w1, w2, w3, w4_words
                 nc.sync.dma_start(out_v[:, 1, e * CH : (e + 1) * CH], res[:, 1, :])
 
         for c in range(NCH - 1):
-            multiply_third(c, 0, CH)
+            for part in range(len(pair[c])):
+                multiply_third(c, part)
         for c in range(NCH - 2):
             last_layer(c)
-        multiply_third(NCH - 1, 0, CH // 2)
+        multiply_third(NCH - 1, 0)
         last_layer(NCH - 2)
-        multiply_third(NCH - 1, CH // 2, CH)
+        multiply_third(NCH - 1, 1)
         last_layer(NCH - 1)

@@ -21,13 +21,17 @@ P = 128
 PACK = 4
 CH = 128
 NCH = V // CH
+HALF_GROUPS = H // PACK // 2
 X_HEAD = 768
-HALF = P // 2
 W1_GPSIMD = 40
 W2_GPSIMD = (16, 24)
 W3_GPSIMD = (30, 22)
 LATE = 384
-SHARE = CH // 2
+PAIR_VECTOR = 2 * CH + CH // 2
+
+HALF_BYTES = PACK * H // 2 * 4
+RAW2_AT = (0, 2 * HALF_BYTES)
+RAW3_AT = (3 * HALF_BYTES, 4 * HALF_BYTES)
 
 
 def tile_picked_trilin_relu_p_kernel(tc, x_words, x_scales, w1, w2, w3, w4_words, w4_scales, offs, out):
@@ -40,7 +44,7 @@ def tile_picked_trilin_relu_p_kernel(tc, x_words, x_scales, w1, w2, w3, w4_words
         offsets = keep.tile([P, S // 16], U16, name="offsets")
         nc.sync.dma_start(offsets[:], offs)
 
-        def load_scales(name, src, width):
+        def load_plane(name, src, width):
             plane = keep.tile([P, width], U8, name=name, align_bytes=64)
             nc.vector.memset(plane[:].bitcast(I32), 0)
             rows = src[0].bitcast(I32).rearrange("(q r) c -> r q c", r=4)
@@ -52,39 +56,39 @@ def tile_picked_trilin_relu_p_kernel(tc, x_words, x_scales, w1, w2, w3, w4_words
             nc.sync.dma_start(raw[:], w.rearrange("(p j) c -> p j c", j=PACK)[:, :, c0 : c0 + raw.shape[2]])
             return raw
 
+        def load_halves(name, w, at):
+            return [
+                load_columns(
+                    shared.tile([P, PACK, H // 2], F32, name="%s%d" % (name, h), align_bytes=64, offset=at[h]), w, h * H // 2
+                )
+                for h in range(2)
+            ]
+
         x_table = keep.tile([P, T], U32, name="x_table", align_bytes=64)
         x_src = x_words[0].rearrange("p c r -> p (c r)").bitcast(I32)
         nc.sync.dma_start(x_table[:, :X_HEAD].bitcast(I32), x_src[:, :X_HEAD])
-        x_plane = load_scales("x_plane", x_scales, T)
+        x_plane = load_plane("x_plane", x_scales, T)
         raw1 = load_columns(keep.tile([P, PACK, H], F32, name="raw1", align_bytes=64), w1, 0)
         nc.sync.dma_start(x_table[:, X_HEAD:].bitcast(I32), x_src[:, X_HEAD:])
-        raw2 = [
-            load_columns(shared.tile([P, PACK, H // 2], F32, name="raw2%d" % h, align_bytes=64, offset=8192 * h), w2, h * H // 2)
-            for h in range(2)
-        ]
-        raw3 = [
-            load_columns(shared.tile([P, PACK, H // 2], F32, name="raw3%d" % h, align_bytes=64, offset=12288 + 4096 * h), w3, h * H // 2)
-            for h in range(2)
-        ]
+        raw2 = load_halves("raw2", w2, RAW2_AT)
+        raw3 = load_halves("raw3", w3, RAW3_AT)
         w4_codes = keep.tile([P, 2 * N], U8, name="w4_codes", align_bytes=64)
         nc.sync.dma_start(w4_codes[:].bitcast(I32), w4_words[0].bitcast(I32))
-        w4_plane = load_scales("w4_plane", w4_scales, N)
+        w4_plane = load_plane("w4_plane", w4_scales, N)
 
         grouped = [keep.tile([P, PACK, P, PACK], BF16, name="grouped", align_bytes=64) for d in range(3)]
         w_codes = [keep.tile([P, H], U32, name="w_codes%d" % d, align_bytes=64) for d in range(3)]
         w_plane = [keep.tile([P, H], U8, name="w_plane%d" % d, align_bytes=64) for d in range(3)]
         picked_plane = keep.tile([P, S], U8, name="picked_plane", align_bytes=64)
 
-        def cast(d, raw, m0, split):
+        def round_weight(d, raw, m0, split):
             groups = raw.shape[2] // PACK
-            if split > 0:
-                src = raw[:].rearrange("p j (m t) -> p m t j", t=PACK)[:, :split]
-                dst = grouped[d][:].rearrange("p t m j -> p m t j")[:, m0 : m0 + split]
-                nc.gpsimd.tensor_scalar(dst, src, 1.0, 0.0, MULT, ADD)
-            if split < groups:
-                src = raw[:].rearrange("p j (m t) -> p m j t", t=PACK)[:, split:]
-                dst = grouped[d][:].rearrange("p t m j -> p m j t")[:, m0 + split : m0 + groups]
-                nc.scalar.copy(out=dst, in_=src)
+            src = raw[:].rearrange("p j (m t) -> p m t j", t=PACK)[:, :split]
+            dst = grouped[d][:].rearrange("p t m j -> p m t j")[:, m0 : m0 + split]
+            nc.gpsimd.tensor_scalar(dst, src, 1.0, 0.0, MULT, ADD)
+            src = raw[:].rearrange("p j (m t) -> p m j t", t=PACK)[:, split:]
+            dst = grouped[d][:].rearrange("p t m j -> p m j t")[:, m0 + split : m0 + groups]
+            nc.scalar.copy(out=dst, in_=src)
 
         def quantize_weight(d, t0, t1):
             nc.vector.quantize_mx(
@@ -93,101 +97,93 @@ def tile_picked_trilin_relu_p_kernel(tc, x_words, x_scales, w1, w2, w3, w4_words
                 in_=grouped[d][:, t0:t1].rearrange("p t m j -> p (t m j)"),
             )
 
-        def product(d, c, tag):
-            bank = psum.tile([P, PACK, CH], F32, name="bank", tag=tag)
-            for t in range(PACK):
-                nc.tensor.matmul_mx(
-                    out=bank[:, t, :],
-                    lhsT=w_codes[d][:, t * P : (t + 1) * P].bitcast(FP8X4),
-                    lhsT_scale=w_plane[d][:, t * P : (t + 1) * P],
-                    rhs=where[d * V + c * CH].bitcast(FP8X4),
-                    rhs_scale=picked_plane[:, d * V + c * CH : d * V + (c + 1) * CH],
-                    start=True,
-                    stop=True,
-                )
-            return bank[:].rearrange("p t v -> p v t")
-
-        nc.vector.tensor_copy(picked_plane[:], x_plane[:].indirect(offsets[:]))
-        where = {}
+        picked_words = {}
 
         def gather_words(tile, runs):
             col = 0
             for e0, e1 in runs:
                 nc.vector.tensor_copy(tile[:, col : col + e1 - e0], x_table[:].indirect(offsets[:, e0 // 16 : e1 // 16]))
                 for e in range(e0, e1, CH):
-                    where[e] = tile[:, col + e - e0 : col + e - e0 + CH]
+                    picked_words[e] = tile[:, col + e - e0 : col + e - e0 + CH]
                 col += e1 - e0
 
-        def columns(tile, c):
-            return tile[:, c * CH * PACK : (c + 1) * CH * PACK].rearrange("p (v t) -> p v t", t=PACK)
+        def product(d, c, tag):
+            bank = psum.tile([P, PACK, CH], F32, name="bank", tag=tag)
+            e = d * V + c * CH
+            for t in range(PACK):
+                nc.tensor.matmul_mx(
+                    out=bank[:, t, :],
+                    lhsT=w_codes[d][:, t * P : (t + 1) * P].bitcast(FP8X4),
+                    lhsT_scale=w_plane[d][:, t * P : (t + 1) * P],
+                    rhs=picked_words[e].bitcast(FP8X4),
+                    rhs_scale=picked_plane[:, e : e + CH],
+                    start=True,
+                    stop=True,
+                )
+            return bank[:].rearrange("p t v -> p v t")
 
+        def by_triple(tile):
+            return tile[:].rearrange("p (v t) -> p v t", t=PACK)
+
+        nc.vector.tensor_copy(picked_plane[:], x_plane[:].indirect(offsets[:]))
         picked_early = keep.tile([P, V // 2], U32, name="picked_early", align_bytes=64)
         gather_words(picked_early, [(0, V // 2)])
-        cast(0, raw1, 0, W1_GPSIMD)
+        round_weight(0, raw1, 0, W1_GPSIMD)
         quantize_weight(0, 0, PACK)
         picked = keep.tile([P, S - LATE - V // 2], U32, name="picked", tag="raw1", align_bytes=64)
         gather_words(picked, [(V // 2, V), (V, S - LATE)])
         first_bank = [product(0, c, "lo%d" % c) for c in range(NCH)]
+
         for h in range(2):
-            cast(1, raw2[h], h * HALF, W2_GPSIMD[h])
-        head = shared.tile([P, 2 * CH * PACK], F32, name="head", align_bytes=64, offset=0)
-        first = [columns(head, c) for c in range(2)]
+            round_weight(1, raw2[h], h * HALF_GROUPS, W2_GPSIMD[h])
+        first_head = shared.tile([P, 2 * CH * PACK], F32, name="first_head", align_bytes=64, offset=RAW2_AT[0])
         for c in range(2):
-            nc.scalar.copy(out=first[c], in_=first_bank[c])
+            nc.scalar.copy(out=by_triple(first_head)[:, c * CH : (c + 1) * CH], in_=first_bank[c])
         quantize_weight(1, 0, PACK // 2)
         quantize_weight(1, PACK // 2, PACK)
-        picked_late = shared.tile([P, LATE], U32, name="picked_late", align_bytes=64, offset=10240)
+        picked_late = shared.tile([P, LATE], U32, name="picked_late", align_bytes=64, offset=RAW2_AT[1] + HALF_BYTES // 2)
         gather_words(picked_late, [(S - LATE, S)])
         second_bank = [product(1, c, "hi%d" % c) for c in range(NCH)]
-        for h in range(2):
-            cast(2, raw3[h], h * HALF, W3_GPSIMD[h])
-        first_tail = keep.tile([P, 2 * CH * PACK], F32, name="first_tail", align_bytes=64)
-        second_tail = keep.tile([P, (CH + SHARE) * PACK], F32, name="second_tail", align_bytes=64)
-        first.extend(columns(first_tail, c) for c in range(2))
-        second_view = second_tail[:].rearrange("p (v t) -> p v t", t=PACK)
-        nc.scalar.copy(out=first[2], in_=first_bank[2])
-        nc.scalar.copy(out=second_view[:, :SHARE], in_=second_bank[2][:, CH - SHARE :])
-        nc.scalar.copy(out=first[3], in_=first_bank[3])
-        nc.scalar.copy(out=second_view[:, SHARE:], in_=second_bank[3])
 
-        pair_head = keep.tile([P, CH * PACK], F32, name="pair_head", align_bytes=64)
-        pair_tail = shared.tile([P, (2 * CH - SHARE) * PACK], F32, name="pair_tail", align_bytes=64, offset=14336)
-        pair_last = keep.tile([P, (CH + SHARE) * PACK], F32, name="pair_last", tag="grouped", align_bytes=64)
-        tail_view = pair_tail[:].rearrange("p (v t) -> p v t", t=PACK)
-        last_view = pair_last[:].rearrange("p (v t) -> p v t", t=PACK)
-        nc.vector.tensor_tensor(columns(pair_head, 0), second_bank[0], first[0], MULT)
+        for h in range(2):
+            round_weight(2, raw3[h], h * HALF_GROUPS, W3_GPSIMD[h])
+        cut = PAIR_VECTOR - 2 * CH
+        first_tail = keep.tile([P, 2 * CH * PACK], F32, name="first_tail", align_bytes=64)
+        second_tail = keep.tile([P, 2 * CH * PACK], F32, name="second_tail", align_bytes=64)
+        nc.scalar.copy(out=by_triple(first_tail)[:, :CH], in_=first_bank[2])
+        nc.scalar.copy(out=by_triple(second_tail)[:, cut:CH], in_=second_bank[2][:, cut:])
+        nc.scalar.copy(out=by_triple(first_tail)[:, CH:], in_=first_bank[3])
+        nc.scalar.copy(out=by_triple(second_tail)[:, CH:], in_=second_bank[3])
+
+        pair0 = keep.tile([P, CH * PACK], F32, name="pair0", align_bytes=64)
+        pair1 = shared.tile([P, CH * PACK], F32, name="pair1", align_bytes=64, offset=RAW3_AT[1] - CH * PACK * 2)
+        pair_tail = keep.tile([P, 2 * CH * PACK], F32, name="pair_tail", tag="grouped", align_bytes=64)
+        nc.vector.tensor_tensor(by_triple(pair0), second_bank[0], by_triple(first_head)[:, :CH], MULT)
         quantize_weight(2, 0, PACK // 2)
         quantize_weight(2, PACK // 2, PACK)
-        nc.vector.tensor_tensor(tail_view[:, :CH], second_bank[1], first[1], MULT)
-        nc.vector.tensor_tensor(tail_view[:, CH:], second_bank[2][:, : CH - SHARE], first[2][:, : CH - SHARE], MULT)
-        cut = SHARE * PACK
-        nc.gpsimd.tensor_tensor(pair_last[:, :cut], second_tail[:, :cut], first_tail[:, CH * PACK - cut : CH * PACK], MULT)
-        nc.gpsimd.tensor_tensor(pair_last[:, cut:], second_tail[:, cut:], first_tail[:, CH * PACK :], MULT)
-        pair = [
-            [(0, CH, columns(pair_head, 0))],
-            [(0, CH, tail_view[:, :CH])],
-            [(0, CH - SHARE, tail_view[:, CH:]), (CH - SHARE, CH, last_view[:, :SHARE])],
-            [(0, CH // 2, last_view[:, SHARE : SHARE + CH // 2]), (CH // 2, CH, last_view[:, SHARE + CH // 2 :])],
-        ]
+        nc.vector.tensor_tensor(by_triple(pair1), second_bank[1], by_triple(first_head)[:, CH:], MULT)
+        nc.vector.tensor_tensor(by_triple(pair_tail)[:, :cut], second_bank[2][:, :cut], by_triple(first_tail)[:, :cut], MULT)
+        for v0, v1 in ((cut, CH), (CH, 2 * CH)):
+            cols = slice(v0 * PACK, v1 * PACK)
+            nc.gpsimd.tensor_tensor(pair_tail[:, cols], second_tail[:, cols], first_tail[:, cols], MULT)
+        pair = [by_triple(pair0), by_triple(pair1), by_triple(pair_tail)[:, :CH], by_triple(pair_tail)[:, CH:]]
 
         out_v = out.rearrange("(u p) v -> p u v", p=P)
-        z = []
-
-        z.extend(keep.tile([P, CH, PACK], BF16, name="z%d" % c, align_bytes=64) for c in range(NCH))
+        z = [keep.tile([P, CH, PACK], BF16, name="z%d" % c, align_bytes=64) for c in range(NCH)]
         third_bank = [product(2, c, "lo%d" % c) for c in range(NCH)]
 
-        def multiply_third(c, part):
-            v0, v1, factor = pair[c][part]
-            nc.vector.tensor_tensor(z[c][:, v0:v1], third_bank[c][:, v0:v1], factor, MULT)
+        def multiply_third(c, v0, v1):
+            nc.vector.tensor_tensor(z[c][:, v0:v1], third_bank[c][:, v0:v1], pair[c][:, v0:v1], MULT)
 
-        def last_layer(e):
-            z_codes = keep.tile([P, CH], U32, name="z_codes%d" % e, align_bytes=64)
-            z_plane = keep.tile([P, CH], U8, name="z_plane%d" % e, align_bytes=64)
-            nc.vector.quantize_mx(
-                out=z_codes[:].bitcast(FP8X4), scales=z_plane[:], in_=z[e][:].rearrange("p v t -> p (v t)")
-            )
-            bank = psum.tile([P, PACK, CH], F32, name="bank", tag="hi%d" % e)
-            banks = [bank, bank if e < NCH - 1 else psum.tile([P, PACK, CH], F32, name="bank", tag="lo0")]
+        def last_product(c, step, banks):
+            z_codes = keep.tile([P, CH], U32, name="z_codes%d" % c, align_bytes=64)
+            z_plane = keep.tile([P, CH], U8, name="z_plane%d" % c, align_bytes=64)
+            for v0 in range(0, CH, step):
+                nc.vector.quantize_mx(
+                    out=z_codes[:, v0 : v0 + step].bitcast(FP8X4),
+                    scales=z_plane[:, v0 : v0 + step],
+                    in_=z[c][:, v0 : v0 + step].rearrange("p v t -> p (v t)"),
+                )
             for u in range(N // P):
                 nc.tensor.matmul_mx(
                     out=banks[u][:, u, :],
@@ -198,22 +194,27 @@ def tile_picked_trilin_relu_p_kernel(tc, x_words, x_scales, w1, w2, w3, w4_words
                     start=True,
                     stop=True,
                 )
-            res = keep.tile([P, N // P, CH], F32, name="res%d" % e, align_bytes=64)
-            if e < NCH - 1:
-                nc.scalar.activation(res[:], bank[:, 0 : N // P, :], RELU)
-                nc.sync.dma_start(out_v[:, :, e * CH : (e + 1) * CH], res[:])
-            else:
-                nc.vector.tensor_scalar_max(res[:, 0, :], banks[0][:, 0, :], 0.0)
-                nc.sync.dma_start(out_v[:, 0, e * CH : (e + 1) * CH], res[:, 0, :])
-                nc.scalar.activation(res[:, 1, :], banks[1][:, 1, :], RELU)
-                nc.sync.dma_start(out_v[:, 1, e * CH : (e + 1) * CH], res[:, 1, :])
 
-        for c in range(NCH - 1):
-            for part in range(len(pair[c])):
-                multiply_third(c, part)
-        for c in range(NCH - 2):
+        def last_layer(c):
+            bank = psum.tile([P, PACK, CH], F32, name="bank", tag="hi%d" % c)
+            last_product(c, CH, [bank, bank])
+            res = keep.tile([P, N // P, CH], F32, name="res%d" % c, align_bytes=64)
+            nc.scalar.activation(res[:], bank[:, 0 : N // P, :], RELU)
+            nc.sync.dma_start(out_v[:, :, c * CH : (c + 1) * CH], res[:])
+
+        last = NCH - 1
+        for c in range(last):
+            multiply_third(c, 0, CH)
+        for c in range(last - 1):
             last_layer(c)
-        multiply_third(NCH - 1, 0)
-        last_layer(NCH - 2)
-        multiply_third(NCH - 1, 1)
-        last_layer(NCH - 1)
+        multiply_third(last, 0, CH // 2)
+        last_layer(last - 1)
+        multiply_third(last, CH // 2, CH)
+
+        banks = [psum.tile([P, PACK, CH], F32, name="bank", tag=tag) for tag in ("hi%d" % last, "lo0")]
+        last_product(last, CH // 2, banks)
+        res = keep.tile([P, N // P, CH], F32, name="res%d" % last, align_bytes=64)
+        nc.vector.tensor_scalar_max(res[:, 0, :], banks[0][:, 0, :], 0.0)
+        nc.sync.dma_start(out_v[:, 0, last * CH :], res[:, 0, :])
+        nc.scalar.activation(res[:, 1, :], banks[1][:, 1, :], RELU)
+        nc.sync.dma_start(out_v[:, 1, last * CH :], res[:, 1, :])

@@ -156,12 +156,12 @@ def tile_picked_trilin_relu_p_kernel(tc, x_words, x_scales, w1, w2, w3, w4_words
         nc.scalar.copy(out=by_triple(second_tail)[:, CH:], in_=second_bank[3])
 
         pair0 = keep.tile([P, CH * PACK], F32, name="pair0", align_bytes=64)
-        pair1 = shared.tile([P, CH * PACK], F32, name="pair1", align_bytes=64, offset=RAW3_AT[1] - CH * PACK * 2)
+        pair1 = keep.tile([P, CH * PACK], F32, name="pair1", align_bytes=64)
         pair_tail = keep.tile([P, 2 * CH * PACK], F32, name="pair_tail", tag="grouped", align_bytes=64)
         nc.vector.tensor_tensor(by_triple(pair0), second_bank[0], by_triple(first_head)[:, :CH], MULT)
+        nc.vector.tensor_tensor(by_triple(pair1), second_bank[1], by_triple(first_head)[:, CH:], MULT)
         quantize_weight(2, 0, PACK // 2)
         quantize_weight(2, PACK // 2, PACK)
-        nc.vector.tensor_tensor(by_triple(pair1), second_bank[1], by_triple(first_head)[:, CH:], MULT)
         nc.vector.tensor_tensor(by_triple(pair_tail)[:, :cut], second_bank[2][:, :cut], by_triple(first_tail)[:, :cut], MULT)
         for v0, v1 in ((cut, CH), (CH, 2 * CH)):
             cols = slice(v0 * PACK, v1 * PACK)

@@ -205,6 +205,16 @@ def tile_picked_trilin_relu_p_kernel(tc, x_words, x_scales, w1, w2, w3, w4_words
         last = NCH - 1
         for c in range(last):
             multiply_third(c, 0, CH)
+        spare = psum.tile([P, PACK * CH], F32, name="bank", tag="lo1")
+        nc.tensor.matmul_mx(
+            out=spare[:],
+            lhsT=w_codes[2][:, :P].bitcast(FP8X4),
+            lhsT_scale=w_plane[2][:, :P],
+            rhs=w_codes[2][:].bitcast(FP8X4),
+            rhs_scale=w_plane[2][:],
+            start=True,
+            stop=True,
+        )
         for c in range(last - 1):
             last_layer(c)
         multiply_third(last, 0, CH // 2)

@@ -25,13 +25,12 @@ HALF_GROUPS = H // PACK // 2
 X_HEAD = 768
 W1_GPSIMD = 40
 W2_GPSIMD = (16, 24)
-W3_GPSIMD = (30, 22)
+W3_GPSIMD = 20
 LATE = 384
 PAIR_VECTOR = 2 * CH + CH // 2
 
 HALF_BYTES = PACK * H // 2 * 4
 RAW2_AT = (0, 2 * HALF_BYTES)
-RAW3_AT = (3 * HALF_BYTES, 4 * HALF_BYTES)
 
 
 def tile_picked_trilin_relu_p_kernel(tc, x_words, x_scales, w1, w2, w3, w4_words, w4_scales, offs, out):
@@ -71,7 +70,10 @@ def tile_picked_trilin_relu_p_kernel(tc, x_words, x_scales, w1, w2, w3, w4_words
         raw1 = load_columns(keep.tile([P, PACK, H], F32, name="raw1", align_bytes=64), w1, 0)
         nc.sync.dma_start(x_table[:, X_HEAD:].bitcast(I32), x_src[:, X_HEAD:])
         raw2 = load_halves("raw2", w2, RAW2_AT)
-        raw3 = load_halves("raw3", w3, RAW3_AT)
+        raw3 = [
+            load_columns(keep.tile([P, PACK, n], F32, name="raw3%d" % c0, align_bytes=64), w3, c0)
+            for c0, n in ((0, H // 2), (H // 2, H // 4), (3 * H // 4, H // 4))
+        ]
         w4_codes = keep.tile([P, 2 * N], U8, name="w4_codes", align_bytes=64)
         nc.sync.dma_start(w4_codes[:].bitcast(I32), w4_words[0].bitcast(I32))
         w4_plane = load_plane("w4_plane", w4_scales, N)
@@ -83,12 +85,14 @@ def tile_picked_trilin_relu_p_kernel(tc, x_words, x_scales, w1, w2, w3, w4_words
 
         def round_weight(d, raw, m0, split):
             groups = raw.shape[2] // PACK
-            src = raw[:].rearrange("p j (m t) -> p m t j", t=PACK)[:, :split]
-            dst = grouped[d][:].rearrange("p t m j -> p m t j")[:, m0 : m0 + split]
-            nc.gpsimd.tensor_scalar(dst, src, 1.0, 0.0, MULT, ADD)
-            src = raw[:].rearrange("p j (m t) -> p m j t", t=PACK)[:, split:]
-            dst = grouped[d][:].rearrange("p t m j -> p m j t")[:, m0 + split : m0 + groups]
-            nc.scalar.copy(out=dst, in_=src)
+            if split > 0:
+                src = raw[:].rearrange("p j (m t) -> p m t j", t=PACK)[:, :split]
+                dst = grouped[d][:].rearrange("p t m j -> p m t j")[:, m0 : m0 + split]
+                nc.gpsimd.tensor_scalar(dst, src, 1.0, 0.0, MULT, ADD)
+            if split < groups:
+                src = raw[:].rearrange("p (a b) (m t) -> p m a t b", b=2, t=PACK)[:, split:]
+                dst = grouped[d][:].rearrange("p t m (a b) -> p m a t b", b=2)[:, m0 + split : m0 + groups]
+                nc.scalar.copy(out=dst, in_=src)
 
         def quantize_weight(d, t0, t1):
             nc.vector.quantize_mx(
@@ -145,8 +149,9 @@ def tile_picked_trilin_relu_p_kernel(tc, x_words, x_scales, w1, w2, w3, w4_words
         gather_words(picked_late, [(S - LATE, S)])
         second_bank = [product(1, c, "hi%d" % c) for c in range(NCH)]
 
-        for h in range(2):
-            round_weight(2, raw3[h], h * HALF_GROUPS, W3_GPSIMD[h])
+        round_weight(2, raw3[0], 0, W3_GPSIMD)
+        round_weight(2, raw3[1], HALF_GROUPS, HALF_GROUPS // 2)
+        round_weight(2, raw3[2], HALF_GROUPS + HALF_GROUPS // 2, 0)
         cut = PAIR_VECTOR - 2 * CH
         first_tail = keep.tile([P, 2 * CH * PACK], F32, name="first_tail", align_bytes=64)
         second_tail = keep.tile([P, 2 * CH * PACK], F32, name="second_tail", align_bytes=64)

@@ -24,7 +24,7 @@ NCH = V // CH
 HALF_GROUPS = H // PACK // 2
 X_HEAD = 768
 W1_GPSIMD = 40
-W2_GPSIMD = (16, 24)
+W2_GPSIMD = 12
 W3_GPSIMD = 20
 LATE = 384
 PAIR_VECTOR = 2 * CH + CH // 2
@@ -55,21 +55,16 @@ def tile_picked_trilin_relu_p_kernel(tc, x_words, x_scales, w1, w2, w3, w4_words
             nc.sync.dma_start(raw[:], w.rearrange("(p j) c -> p j c", j=PACK)[:, :, c0 : c0 + raw.shape[2]])
             return raw
 
-        def load_halves(name, w, at):
-            return [
-                load_columns(
-                    shared.tile([P, PACK, H // 2], F32, name="%s%d" % (name, h), align_bytes=64, offset=at[h]), w, h * H // 2
-                )
-                for h in range(2)
-            ]
-
         x_table = keep.tile([P, T], U32, name="x_table", align_bytes=64)
         x_src = x_words[0].rearrange("p c r -> p (c r)").bitcast(I32)
         nc.sync.dma_start(x_table[:, :X_HEAD].bitcast(I32), x_src[:, :X_HEAD])
         x_plane = load_plane("x_plane", x_scales, T)
         raw1 = load_columns(keep.tile([P, PACK, H], F32, name="raw1", align_bytes=64), w1, 0)
         nc.sync.dma_start(x_table[:, X_HEAD:].bitcast(I32), x_src[:, X_HEAD:])
-        raw2 = load_halves("raw2", w2, RAW2_AT)
+        raw2 = [
+            load_columns(shared.tile([P, PACK, n], F32, name="raw2%d" % c0, align_bytes=64, offset=at), w2, c0)
+            for c0, n, at in ((0, H // 2, RAW2_AT[0]), (H // 2, H // 4, RAW2_AT[1]), (3 * H // 4, H // 4, RAW2_AT[1] + HALF_BYTES // 2))
+        ]
         raw3 = [
             load_columns(keep.tile([P, PACK, n], F32, name="raw3%d" % c0, align_bytes=64), w3, c0)
             for c0, n in ((0, H // 2), (H // 2, H // 4), (3 * H // 4, H // 4))
@@ -138,20 +133,26 @@ def tile_picked_trilin_relu_p_kernel(tc, x_words, x_scales, w1, w2, w3, w4_words
         gather_words(picked, [(V // 2, V), (V, S - LATE)])
         first_bank = [product(0, c, "lo%d" % c) for c in range(NCH)]
 
-        for h in range(2):
-            round_weight(1, raw2[h], h * HALF_GROUPS, W2_GPSIMD[h])
+        round_weight(1, raw2[0], 0, W2_GPSIMD)
+        round_weight(1, raw2[1], HALF_GROUPS, HALF_GROUPS // 2)
+        round_weight(1, raw2[2], HALF_GROUPS + HALF_GROUPS // 2, 0)
         first_head = shared.tile([P, 2 * CH * PACK], F32, name="first_head", align_bytes=64, offset=RAW2_AT[0])
         for c in range(2):
             nc.scalar.copy(out=by_triple(first_head)[:, c * CH : (c + 1) * CH], in_=first_bank[c])
         quantize_weight(1, 0, PACK // 2)
         quantize_weight(1, PACK // 2, PACK)
-        picked_late = shared.tile([P, LATE], U32, name="picked_late", align_bytes=64, offset=RAW2_AT[1] + HALF_BYTES // 2)
+        picked_late = shared.tile([P, LATE], U32, name="picked_late", align_bytes=64, offset=RAW2_AT[1] + HALF_BYTES // 4)
         gather_words(picked_late, [(S - LATE, S)])
-        second_bank = [product(1, c, "hi%d" % c) for c in range(NCH)]
+        second_bank = [product(1, c, "hi%d" % c) for c in range(3)]
 
         round_weight(2, raw3[0], 0, W3_GPSIMD)
         round_weight(2, raw3[1], HALF_GROUPS, HALF_GROUPS // 2)
         round_weight(2, raw3[2], HALF_GROUPS + HALF_GROUPS // 2, 0)
+        pair0 = keep.tile([P, CH * PACK], F32, name="pair0", align_bytes=64)
+        pair1 = keep.tile([P, CH * PACK], F32, name="pair1", align_bytes=64)
+        nc.vector.tensor_tensor(by_triple(pair0), second_bank[0], by_triple(first_head)[:, :CH], MULT)
+        second_bank.append(product(1, 3, "hi0"))
+        nc.vector.tensor_tensor(by_triple(pair1), second_bank[1], by_triple(first_head)[:, CH:], MULT)
         cut = PAIR_VECTOR - 2 * CH
         first_tail = keep.tile([P, 2 * CH * PACK], F32, name="first_tail", align_bytes=64)
         second_tail = keep.tile([P, 2 * CH * PACK], F32, name="second_tail", align_bytes=64)
@@ -160,11 +161,7 @@ def tile_picked_trilin_relu_p_kernel(tc, x_words, x_scales, w1, w2, w3, w4_words
         nc.scalar.copy(out=by_triple(first_tail)[:, CH:], in_=first_bank[3])
         nc.scalar.copy(out=by_triple(second_tail)[:, CH:], in_=second_bank[3])
 
-        pair0 = keep.tile([P, CH * PACK], F32, name="pair0", align_bytes=64)
-        pair1 = keep.tile([P, CH * PACK], F32, name="pair1", align_bytes=64)
         pair_tail = keep.tile([P, 2 * CH * PACK], F32, name="pair_tail", tag="grouped", align_bytes=64)
-        nc.vector.tensor_tensor(by_triple(pair0), second_bank[0], by_triple(first_head)[:, :CH], MULT)
-        nc.vector.tensor_tensor(by_triple(pair1), second_bank[1], by_triple(first_head)[:, CH:], MULT)
         quantize_weight(2, 0, PACK // 2)
         quantize_weight(2, PACK // 2, PACK)
         nc.vector.tensor_tensor(by_triple(pair_tail)[:, :cut], second_bank[2][:, :cut], by_triple(first_tail)[:, :cut], MULT)
@@ -175,7 +172,7 @@ def tile_picked_trilin_relu_p_kernel(tc, x_words, x_scales, w1, w2, w3, w4_words
 
         out_v = out.rearrange("(u p) v -> p u v", p=P)
         z = [keep.tile([P, CH, PACK], BF16, name="z%d" % c, align_bytes=64) for c in range(NCH)]
-        third_bank = [product(2, c, "lo%d" % c) for c in range(NCH)]
+        third_bank = [product(2, c, tag) for c, tag in enumerate(("lo0", "lo1", "hi3", "lo2"))]
 
         def multiply_third(c, v0, v1):
             nc.vector.tensor_tensor(z[c][:, v0:v1], third_bank[c][:, v0:v1], pair[c][:, v0:v1], MULT)
@@ -201,7 +198,7 @@ def tile_picked_trilin_relu_p_kernel(tc, x_words, x_scales, w1, w2, w3, w4_words
                 )
 
         def last_layer(c):
-            bank = psum.tile([P, PACK, CH], F32, name="bank", tag="hi%d" % c)
+            bank = psum.tile([P, PACK, CH], F32, name="bank", tag=("hi1", "hi2", "hi0")[c])
             last_product(c, CH, [bank, bank])
             res = keep.tile([P, N // P, CH], F32, name="res%d" % c, align_bytes=64)
             nc.scalar.activation(res[:], bank[:, 0 : N // P, :], RELU)
@@ -226,7 +223,7 @@ def tile_picked_trilin_relu_p_kernel(tc, x_words, x_scales, w1, w2, w3, w4_words
         last_layer(last - 1)
         multiply_third(last, CH // 2, CH)
 
-        banks = [psum.tile([P, PACK, CH], F32, name="bank", tag=tag) for tag in ("hi%d" % last, "lo0")]
+        banks = [psum.tile([P, PACK, CH], F32, name="bank", tag=tag) for tag in ("lo3", "lo0")]
         last_product(last, CH // 2, banks)
         res = keep.tile([P, N // P, CH], F32, name="res%d" % last, align_bytes=64)
         nc.vector.tensor_scalar_max(res[:, 0, :], banks[0][:, 0, :], 0.0)

@@ -44,7 +44,7 @@ def tile_picked_trilin_relu_p_kernel(tc, x_words, x_scales, w1, w2, w3, w4_words
         nc.sync.dma_start(offsets[:], offs)
 
         def load_plane(name, src, width):
-            plane = keep.tile([P, width], U8, name=name, align_bytes=64)
+            plane = keep.tile([P, width], U8, name=name, align_bytes=256)
             nc.vector.memset(plane[:].bitcast(I32), 0)
             rows = src[0].bitcast(I32).rearrange("(q r) c -> r q c", r=4)
             for r in range(4):
@@ -55,28 +55,28 @@ def tile_picked_trilin_relu_p_kernel(tc, x_words, x_scales, w1, w2, w3, w4_words
             nc.sync.dma_start(raw[:], w.rearrange("(p j) c -> p j c", j=PACK)[:, :, c0 : c0 + raw.shape[2]])
             return raw
 
-        x_table = keep.tile([P, T], U32, name="x_table", align_bytes=64)
+        x_table = keep.tile([P, T], U32, name="x_table", align_bytes=256)
         x_src = x_words[0].rearrange("p c r -> p (c r)").bitcast(I32)
         nc.sync.dma_start(x_table[:, :X_HEAD].bitcast(I32), x_src[:, :X_HEAD])
         x_plane = load_plane("x_plane", x_scales, T)
-        raw1 = load_columns(keep.tile([P, PACK, H], F32, name="raw1", align_bytes=64), w1, 0)
+        raw1 = load_columns(keep.tile([P, PACK, H], F32, name="raw1", align_bytes=256), w1, 0)
         nc.sync.dma_start(x_table[:, X_HEAD:].bitcast(I32), x_src[:, X_HEAD:])
         raw2 = [
-            load_columns(shared.tile([P, PACK, n], F32, name="raw2%d" % c0, align_bytes=64, offset=at), w2, c0)
+            load_columns(shared.tile([P, PACK, n], F32, name="raw2%d" % c0, align_bytes=256, offset=at), w2, c0)
             for c0, n, at in ((0, H // 2, RAW2_AT[0]), (H // 2, H // 4, RAW2_AT[1]), (3 * H // 4, H // 4, RAW2_AT[1] + HALF_BYTES // 2))
         ]
         raw3 = [
-            load_columns(keep.tile([P, PACK, n], F32, name="raw3%d" % c0, align_bytes=64), w3, c0)
+            load_columns(keep.tile([P, PACK, n], F32, name="raw3%d" % c0, align_bytes=256), w3, c0)
             for c0, n in ((0, H // 2), (H // 2, H // 4), (3 * H // 4, H // 4))
         ]
-        w4_codes = keep.tile([P, 2 * N], U8, name="w4_codes", align_bytes=64)
+        w4_codes = keep.tile([P, 2 * N], U8, name="w4_codes", align_bytes=256)
         nc.sync.dma_start(w4_codes[:].bitcast(I32), w4_words[0].bitcast(I32))
         w4_plane = load_plane("w4_plane", w4_scales, N)
 
-        grouped = [keep.tile([P, PACK, P, PACK], BF16, name="grouped", align_bytes=64) for d in range(3)]
-        w_codes = [keep.tile([P, H], U32, name="w_codes%d" % d, align_bytes=64) for d in range(3)]
-        w_plane = [keep.tile([P, H], U8, name="w_plane%d" % d, align_bytes=64) for d in range(3)]
-        picked_plane = keep.tile([P, S], U8, name="picked_plane", align_bytes=64)
+        grouped = [keep.tile([P, PACK, P, PACK], BF16, name="grouped", align_bytes=256) for d in range(3)]
+        w_codes = [keep.tile([P, H], U32, name="w_codes%d" % d, align_bytes=256) for d in range(3)]
+        w_plane = [keep.tile([P, H], U8, name="w_plane%d" % d, align_bytes=256) for d in range(3)]
+        picked_plane = keep.tile([P, S], U8, name="picked_plane", align_bytes=256)
 
         def round_weight(d, raw, m0, split):
             groups = raw.shape[2] // PACK
@@ -125,43 +125,43 @@ def tile_picked_trilin_relu_p_kernel(tc, x_words, x_scales, w1, w2, w3, w4_words
             return tile[:].rearrange("p (v t) -> p v t", t=PACK)
 
         nc.vector.tensor_copy(picked_plane[:], x_plane[:].indirect(offsets[:]))
-        picked_early = keep.tile([P, V // 2], U32, name="picked_early", align_bytes=64)
+        picked_early = keep.tile([P, V // 2], U32, name="picked_early", align_bytes=256)
         gather_words(picked_early, [(0, V // 2)])
         round_weight(0, raw1, 0, W1_GPSIMD)
         quantize_weight(0, 0, PACK)
-        picked = keep.tile([P, S - LATE - V // 2], U32, name="picked", tag="raw1", align_bytes=64)
+        picked = keep.tile([P, S - LATE - V // 2], U32, name="picked", tag="raw1", align_bytes=256)
         gather_words(picked, [(V // 2, V), (V, S - LATE)])
         first_bank = [product(0, c, "lo%d" % c) for c in range(NCH)]
 
         round_weight(1, raw2[0], 0, W2_GPSIMD)
         round_weight(1, raw2[1], HALF_GROUPS, HALF_GROUPS // 2)
         round_weight(1, raw2[2], HALF_GROUPS + HALF_GROUPS // 2, 0)
-        first_head = shared.tile([P, 2 * CH * PACK], F32, name="first_head", align_bytes=64, offset=RAW2_AT[0])
+        first_head = shared.tile([P, 2 * CH * PACK], F32, name="first_head", align_bytes=256, offset=RAW2_AT[0])
         for c in range(2):
             nc.scalar.copy(out=by_triple(first_head)[:, c * CH : (c + 1) * CH], in_=first_bank[c])
         quantize_weight(1, 0, PACK // 2)
         quantize_weight(1, PACK // 2, PACK)
-        picked_late = shared.tile([P, LATE], U32, name="picked_late", align_bytes=64, offset=RAW2_AT[1] + HALF_BYTES // 4)
+        picked_late = shared.tile([P, LATE], U32, name="picked_late", align_bytes=256, offset=RAW2_AT[1] + HALF_BYTES // 4)
         gather_words(picked_late, [(S - LATE, S)])
         second_bank = [product(1, c, "hi%d" % c) for c in range(3)]
 
         round_weight(2, raw3[0], 0, W3_GPSIMD)
         round_weight(2, raw3[1], HALF_GROUPS, HALF_GROUPS // 2)
         round_weight(2, raw3[2], HALF_GROUPS + HALF_GROUPS // 2, 0)
-        pair0 = keep.tile([P, CH * PACK], F32, name="pair0", align_bytes=64)
-        pair1 = keep.tile([P, CH * PACK], F32, name="pair1", align_bytes=64)
+        pair0 = keep.tile([P, CH * PACK], F32, name="pair0", align_bytes=256)
+        pair1 = keep.tile([P, CH * PACK], F32, name="pair1", align_bytes=256)
         nc.vector.tensor_tensor(by_triple(pair0), second_bank[0], by_triple(first_head)[:, :CH], MULT)
         second_bank.append(product(1, 3, "hi0"))
         nc.vector.tensor_tensor(by_triple(pair1), second_bank[1], by_triple(first_head)[:, CH:], MULT)
         cut = PAIR_VECTOR - 2 * CH
-        first_tail = keep.tile([P, 2 * CH * PACK], F32, name="first_tail", align_bytes=64)
-        second_tail = keep.tile([P, 2 * CH * PACK], F32, name="second_tail", align_bytes=64)
+        first_tail = keep.tile([P, 2 * CH * PACK], F32, name="first_tail", align_bytes=256)
+        second_tail = keep.tile([P, 2 * CH * PACK], F32, name="second_tail", align_bytes=256)
         nc.scalar.copy(out=by_triple(first_tail)[:, :CH], in_=first_bank[2])
         nc.scalar.copy(out=by_triple(second_tail)[:, cut:CH], in_=second_bank[2][:, cut:])
         nc.scalar.copy(out=by_triple(first_tail)[:, CH:], in_=first_bank[3])
         nc.scalar.copy(out=by_triple(second_tail)[:, CH:], in_=second_bank[3])
 
-        pair_tail = keep.tile([P, 2 * CH * PACK], F32, name="pair_tail", tag="grouped", align_bytes=64)
+        pair_tail = keep.tile([P, 2 * CH * PACK], F32, name="pair_tail", tag="grouped", align_bytes=256)
         quantize_weight(2, 0, PACK // 2)
         quantize_weight(2, PACK // 2, PACK)
         nc.vector.tensor_tensor(by_triple(pair_tail)[:, :cut], second_bank[2][:, :cut], by_triple(first_tail)[:, :cut], MULT)
@@ -171,15 +171,15 @@ def tile_picked_trilin_relu_p_kernel(tc, x_words, x_scales, w1, w2, w3, w4_words
         pair = [by_triple(pair0), by_triple(pair1), by_triple(pair_tail)[:, :CH], by_triple(pair_tail)[:, CH:]]
 
         out_v = out.rearrange("(u p) v -> p u v", p=P)
-        z = [keep.tile([P, CH, PACK], BF16, name="z%d" % c, align_bytes=64) for c in range(NCH)]
+        z = [keep.tile([P, CH, PACK], BF16, name="z%d" % c, align_bytes=256) for c in range(NCH)]
         third_bank = [product(2, c, tag) for c, tag in enumerate(("lo0", "lo1", "hi3", "lo2"))]
 
         def multiply_third(c, v0, v1):
             nc.vector.tensor_tensor(z[c][:, v0:v1], third_bank[c][:, v0:v1], pair[c][:, v0:v1], MULT)
 
         def last_product(c, step, banks):
-            z_codes = keep.tile([P, CH], U32, name="z_codes%d" % c, align_bytes=64)
-            z_plane = keep.tile([P, CH], U8, name="z_plane%d" % c, align_bytes=64)
+            z_codes = keep.tile([P, CH], U32, name="z_codes%d" % c, align_bytes=256)
+            z_plane = keep.tile([P, CH], U8, name="z_plane%d" % c, align_bytes=256)
             for v0 in range(0, CH, step):
                 nc.vector.quantize_mx(
                     out=z_codes[:, v0 : v0 + step].bitcast(FP8X4),
@@ -200,7 +200,7 @@ def tile_picked_trilin_relu_p_kernel(tc, x_words, x_scales, w1, w2, w3, w4_words
         def last_layer(c):
             bank = psum.tile([P, PACK, CH], F32, name="bank", tag=("hi1", "hi2", "hi0")[c])
             last_product(c, CH, [bank, bank])
-            res = keep.tile([P, N // P, CH], F32, name="res%d" % c, align_bytes=64)
+            res = keep.tile([P, N // P, CH], F32, name="res%d" % c, align_bytes=256)
             nc.scalar.activation(res[:], bank[:, 0 : N // P, :], RELU)
             nc.sync.dma_start(out_v[:, :, c * CH : (c + 1) * CH], res[:])
 
@@ -225,7 +225,7 @@ def tile_picked_trilin_relu_p_kernel(tc, x_words, x_scales, w1, w2, w3, w4_words
 
         banks = [psum.tile([P, PACK, CH], F32, name="bank", tag=tag) for tag in ("lo3", "lo0")]
         last_product(last, CH // 2, banks)
-        res = keep.tile([P, N // P, CH], F32, name="res%d" % last, align_bytes=64)
+        res = keep.tile([P, N // P, CH], F32, name="res%d" % last, align_bytes=256)
         nc.vector.tensor_scalar_max(res[:, 0, :], banks[0][:, 0, :], 0.0)
         nc.sync.dma_start(out_v[:, 0, last * CH :], res[:, 0, :])
         nc.scalar.activation(res[:, 1, :], banks[1][:, 1, :], RELU)

@@ -24,9 +24,9 @@ NCH = V // CH
 HALF_GROUPS = H // PACK // 2
 X_HEAD = 768
 W1_GPSIMD = 40
-W2_GPSIMD = 12
+W2_GPSIMD = 32
 W3_GPSIMD = 20
-LATE = 384
+LATE = 512
 PAIR_VECTOR = 2 * CH + CH // 2
 
 HALF_BYTES = PACK * H // 2 * 4
@@ -73,29 +73,33 @@ def tile_picked_trilin_relu_p_kernel(tc, x_words, x_scales, w1, w2, w3, w4_words
         nc.sync.dma_start(w4_codes[:].bitcast(I32), w4_words[0].bitcast(I32))
         w4_plane = load_plane("w4_plane", w4_scales, N)
 
-        grouped = [keep.tile([P, PACK, P, PACK], BF16, name="grouped", align_bytes=256) for d in range(3)]
+        rounded1 = keep.tile([P, PACK, P, PACK], BF16, name="rounded1", tag="grouped", align_bytes=256)
+        low2 = keep.tile([P, PACK // 2, P, PACK], BF16, name="low2", align_bytes=256)
+        high2 = keep.tile([P, PACK // 2, P, PACK], BF16, name="high2", tag="grouped", align_bytes=256)
+        rounded3 = keep.tile([P, PACK, P, PACK], BF16, name="rounded3", tag="grouped", align_bytes=256)
         w_codes = [keep.tile([P, H], U32, name="w_codes%d" % d, align_bytes=256) for d in range(3)]
         w_plane = [keep.tile([P, H], U8, name="w_plane%d" % d, align_bytes=256) for d in range(3)]
         picked_plane = keep.tile([P, S], U8, name="picked_plane", align_bytes=256)
 
-        def round_weight(d, raw, m0, split):
-            groups = raw.shape[2] // PACK
-            if split > 0:
-                src = raw[:].rearrange("p j (m t) -> p m t j", t=PACK)[:, :split]
-                dst = grouped[d][:].rearrange("p t m j -> p m t j")[:, m0 : m0 + split]
-                nc.gpsimd.tensor_scalar(dst, src, 1.0, 0.0, MULT, ADD)
-            if split < groups:
-                src = raw[:].rearrange("p (a b) (m t) -> p m a t b", b=2, t=PACK)[:, split:]
-                dst = grouped[d][:].rearrange("p t m (a b) -> p m a t b", b=2)[:, m0 + split : m0 + groups]
-                nc.scalar.copy(out=dst, in_=src)
+        def round_on_gpsimd(dst, raw, m0, groups, places):
+            src = raw[:].rearrange("p j (m t) -> p m t j", t=PACK)[:, groups, places]
+            dst = dst.rearrange("p t m j -> p m t j")[:, m0 + groups.start : m0 + groups.stop]
+            nc.gpsimd.tensor_scalar(dst, src, 1.0, 0.0, MULT, ADD)
 
-        def quantize_weight(d, t0, t1):
+        def round_on_scalar(dst, raw, m0, groups, places):
+            src = raw[:].rearrange("p (a b) (m t) -> p m a t b", b=2, t=PACK)[:, groups, :, places]
+            dst = dst.rearrange("p t m (a b) -> p m a t b", b=2)[:, m0 + groups.start : m0 + groups.stop]
+            nc.scalar.copy(out=dst, in_=src)
+
+        def quantize_weight(d, t0, rounded):
+            t1 = t0 + rounded.shape[1]
             nc.vector.quantize_mx(
                 out=w_codes[d][:, t0 * P : t1 * P].bitcast(FP8X4),
                 scales=w_plane[d][:, t0 * P : t1 * P],
-                in_=grouped[d][:, t0:t1].rearrange("p t m j -> p (t m j)"),
+                in_=rounded.rearrange("p t m j -> p (t m j)"),
             )
 
+        every, low, high = slice(0, 4), slice(0, 2), slice(2, 4)
         picked_words = {}
 
         def gather_words(tile, runs):
@@ -127,27 +131,33 @@ def tile_picked_trilin_relu_p_kernel(tc, x_words, x_scales, w1, w2, w3, w4_words
         nc.vector.tensor_copy(picked_plane[:], x_plane[:].indirect(offsets[:]))
         picked_early = keep.tile([P, V // 2], U32, name="picked_early", align_bytes=256)
         gather_words(picked_early, [(0, V // 2)])
-        round_weight(0, raw1, 0, W1_GPSIMD)
-        quantize_weight(0, 0, PACK)
+        round_on_gpsimd(rounded1[:], raw1, 0, slice(0, W1_GPSIMD), every)
+        round_on_scalar(rounded1[:], raw1, 0, slice(W1_GPSIMD, P), every)
+        quantize_weight(0, 0, rounded1[:])
         picked = keep.tile([P, S - LATE - V // 2], U32, name="picked", tag="raw1", align_bytes=256)
         gather_words(picked, [(V // 2, V), (V, S - LATE)])
         first_bank = [product(0, c, "lo%d" % c) for c in range(NCH)]
 
-        round_weight(1, raw2[0], 0, W2_GPSIMD)
-        round_weight(1, raw2[1], HALF_GROUPS, HALF_GROUPS // 2)
-        round_weight(1, raw2[2], HALF_GROUPS + HALF_GROUPS // 2, 0)
+        round_on_scalar(low2[:], raw2[0], 0, slice(0, 64), low)
+        round_on_gpsimd(high2[:], raw2[0], 0, slice(0, W2_GPSIMD), high)
+        round_on_scalar(high2[:], raw2[0], 0, slice(W2_GPSIMD, 64), high)
+        round_on_scalar(low2[:], raw2[1], 64, slice(0, 32), low)
+        round_on_gpsimd(high2[:], raw2[1], 64, slice(0, 32), high)
+        round_on_scalar(low2[:], raw2[2], 96, slice(0, 32), low)
+        round_on_scalar(high2[:], raw2[2], 96, slice(0, 32), high)
         first_head = shared.tile([P, 2 * CH * PACK], F32, name="first_head", align_bytes=256, offset=RAW2_AT[0])
         for c in range(2):
             nc.scalar.copy(out=by_triple(first_head)[:, c * CH : (c + 1) * CH], in_=first_bank[c])
-        quantize_weight(1, 0, PACK // 2)
-        quantize_weight(1, PACK // 2, PACK)
-        picked_late = shared.tile([P, LATE], U32, name="picked_late", align_bytes=256, offset=RAW2_AT[1] + HALF_BYTES // 4)
-        gather_words(picked_late, [(S - LATE, S)])
+        quantize_weight(1, 0, low2[:])
+        quantize_weight(1, 2, high2[:])
+        picked_late = shared.tile([P, LATE - CH], U32, name="picked_late", align_bytes=256, offset=RAW2_AT[1] + HALF_BYTES // 4)
+        gather_words(picked_late, [(S - LATE, S - CH)])
         second_bank = [product(1, c, "hi%d" % c) for c in range(3)]
 
-        round_weight(2, raw3[0], 0, W3_GPSIMD)
-        round_weight(2, raw3[1], HALF_GROUPS, HALF_GROUPS // 2)
-        round_weight(2, raw3[2], HALF_GROUPS + HALF_GROUPS // 2, 0)
+        round_on_gpsimd(rounded3[:], raw3[0], 0, slice(0, W3_GPSIMD), every)
+        round_on_scalar(rounded3[:], raw3[0], 0, slice(W3_GPSIMD, 64), every)
+        round_on_gpsimd(rounded3[:], raw3[1], 64, slice(0, 32), every)
+        round_on_scalar(rounded3[:], raw3[2], 96, slice(0, 32), every)
         pair0 = keep.tile([P, CH * PACK], F32, name="pair0", align_bytes=256)
         pair1 = keep.tile([P, CH * PACK], F32, name="pair1", align_bytes=256)
         nc.vector.tensor_tensor(by_triple(pair0), second_bank[0], by_triple(first_head)[:, :CH], MULT)
@@ -162,8 +172,10 @@ def tile_picked_trilin_relu_p_kernel(tc, x_words, x_scales, w1, w2, w3, w4_words
         nc.scalar.copy(out=by_triple(second_tail)[:, CH:], in_=second_bank[3])
 
         pair_tail = keep.tile([P, 2 * CH * PACK], F32, name="pair_tail", tag="grouped", align_bytes=256)
-        quantize_weight(2, 0, PACK // 2)
-        quantize_weight(2, PACK // 2, PACK)
+        quantize_weight(2, 0, rounded3[:, low])
+        quantize_weight(2, 2, rounded3[:, high])
+        picked_last = keep.tile([P, CH], U32, name="picked_last", tag="raw3384", align_bytes=256)
+        gather_words(picked_last, [(S - CH, S)])
         nc.vector.tensor_tensor(by_triple(pair_tail)[:, :cut], second_bank[2][:, :cut], by_triple(first_tail)[:, :cut], MULT)
         for v0, v1 in ((cut, CH), (CH, 2 * CH)):
             cols = slice(v0 * PACK, v1 * PACK)

@@ -23,7 +23,7 @@ CH = 128
 NCH = V // CH
 HALF_GROUPS = H // PACK // 2
 X_HEAD = 768
-W1_GPSIMD = 40
+W1_GPSIMD = 32
 W2_GPSIMD = 32
 W3_GPSIMD = 20
 LATE = 512

@@ -22,8 +22,8 @@ PACK = 4
 CH = 128
 NCH = V // CH
 HALF_GROUPS = H // PACK // 2
-X_HEAD = 768
-W1_GPSIMD = 32
+X_HEAD = 576
+W1_GPSIMD = 28
 W2_GPSIMD = 32
 W3_GPSIMD = 20
 LATE = 512

from contextlib import ExitStack

import concourse.mybir as mybir

K, T, S, V, H, N = 512, 2048, 1536, 512, 512, 256
FLOPS = 2 * K * H * V * 3 + 2 * H * N * V

F32 = mybir.dt.float32
BF16 = mybir.dt.bfloat16
I32 = mybir.dt.int32
U32 = mybir.dt.uint32
U16 = mybir.dt.uint16
U8 = mybir.dt.uint8
FP8X4 = mybir.dt.float8_e4m3fn_x4
FP4X4 = mybir.dt.float4_e2m1fn_x4
MULT = mybir.AluOpType.mult
ADD = mybir.AluOpType.add
RELU = mybir.ActivationFunctionType.Relu

P = 128
PACK = 4
CH = 128
NCH = V // CH
HALF_GROUPS = H // PACK // 2
X_HEAD = 576
W1_GPSIMD = 28
W2_GPSIMD = 32
W3_GPSIMD = 20
LATE = 512
PAIR_VECTOR = 2 * CH + CH // 2

HALF_BYTES = PACK * H // 2 * 4
RAW2_AT = (0, 2 * HALF_BYTES)


def tile_picked_trilin_relu_p_kernel(tc, x_words, x_scales, w1, w2, w3, w4_words, w4_scales, offs, out):
    nc = tc.nc
    with ExitStack() as ctx:
        keep = ctx.enter_context(tc.tile_pool(name="keep", bufs=1))
        shared = ctx.enter_context(tc.tile_pool(name="shared", bufs=1))
        psum = ctx.enter_context(tc.psum_pool(name="psum", bufs=1))

        offsets = keep.tile([P, S // 16], U16, name="offsets")
        nc.sync.dma_start(offsets[:], offs)

        def load_plane(name, src, width):
            plane = keep.tile([P, width], U8, name=name, align_bytes=256)
            nc.vector.memset(plane[:].bitcast(I32), 0)
            rows = src[0].bitcast(I32).rearrange("(q r) c -> r q c", r=4)
            for r in range(4):
                nc.sync.dma_start(plane[r:P:32, :].bitcast(I32), rows[r])
            return plane

        def load_columns(raw, w, c0):
            nc.sync.dma_start(raw[:], w.rearrange("(p j) c -> p j c", j=PACK)[:, :, c0 : c0 + raw.shape[2]])
            return raw

        x_table = keep.tile([P, T], U32, name="x_table", align_bytes=256)
        x_src = x_words[0].rearrange("p c r -> p (c r)").bitcast(I32)
        nc.sync.dma_start(x_table[:, :X_HEAD].bitcast(I32), x_src[:, :X_HEAD])
        x_plane = load_plane("x_plane", x_scales, T)
        raw1 = load_columns(keep.tile([P, PACK, H], F32, name="raw1", align_bytes=256), w1, 0)
        nc.sync.dma_start(x_table[:, X_HEAD:].bitcast(I32), x_src[:, X_HEAD:])
        raw2 = [
            load_columns(shared.tile([P, PACK, n], F32, name="raw2%d" % c0, align_bytes=256, offset=at), w2, c0)
            for c0, n, at in ((0, H // 2, RAW2_AT[0]), (H // 2, H // 4, RAW2_AT[1]), (3 * H // 4, H // 4, RAW2_AT[1] + HALF_BYTES // 2))
        ]
        raw3 = [
            load_columns(keep.tile([P, PACK, n], F32, name="raw3%d" % c0, align_bytes=256), w3, c0)
            for c0, n in ((0, H // 2), (H // 2, H // 4), (3 * H // 4, H // 4))
        ]
        w4_codes = keep.tile([P, 2 * N], U8, name="w4_codes", align_bytes=256)
        nc.sync.dma_start(w4_codes[:].bitcast(I32), w4_words[0].bitcast(I32))
        w4_plane = load_plane("w4_plane", w4_scales, N)

        rounded1 = keep.tile([P, PACK, P, PACK], BF16, name="rounded1", tag="grouped", align_bytes=256)
        low2 = keep.tile([P, PACK // 2, P, PACK], BF16, name="low2", align_bytes=256)
        high2 = keep.tile([P, PACK // 2, P, PACK], BF16, name="high2", tag="grouped", align_bytes=256)
        rounded3 = keep.tile([P, PACK, P, PACK], BF16, name="rounded3", tag="grouped", align_bytes=256)
        w_codes = [keep.tile([P, H], U32, name="w_codes%d" % d, align_bytes=256) for d in range(3)]
        w_plane = [keep.tile([P, H], U8, name="w_plane%d" % d, align_bytes=256) for d in range(3)]
        picked_plane = keep.tile([P, S], U8, name="picked_plane", align_bytes=256)

        def round_on_gpsimd(dst, raw, m0, groups, places):
            src = raw[:].rearrange("p j (m t) -> p m t j", t=PACK)[:, groups, places]
            dst = dst.rearrange("p t m j -> p m t j")[:, m0 + groups.start : m0 + groups.stop]
            nc.gpsimd.tensor_scalar(dst, src, 1.0, 0.0, MULT, ADD)

        def round_on_scalar(dst, raw, m0, groups, places):
            src = raw[:].rearrange("p (a b) (m t) -> p m a t b", b=2, t=PACK)[:, groups, :, places]
            dst = dst.rearrange("p t m (a b) -> p m a t b", b=2)[:, m0 + groups.start : m0 + groups.stop]
            nc.scalar.copy(out=dst, in_=src)

        def quantize_weight(d, t0, rounded):
            t1 = t0 + rounded.shape[1]
            nc.vector.quantize_mx(
                out=w_codes[d][:, t0 * P : t1 * P].bitcast(FP8X4),
                scales=w_plane[d][:, t0 * P : t1 * P],
                in_=rounded.rearrange("p t m j -> p (t m j)"),
            )

        every, low, high = slice(0, 4), slice(0, 2), slice(2, 4)
        picked_words = {}

        def gather_words(tile, runs):
            col = 0
            for e0, e1 in runs:
                nc.vector.tensor_copy(tile[:, col : col + e1 - e0], x_table[:].indirect(offsets[:, e0 // 16 : e1 // 16]))
                for e in range(e0, e1, CH):
                    picked_words[e] = tile[:, col + e - e0 : col + e - e0 + CH]
                col += e1 - e0

        def product(d, c, tag):
            bank = psum.tile([P, PACK, CH], F32, name="bank", tag=tag)
            e = d * V + c * CH
            for t in range(PACK):
                nc.tensor.matmul_mx(
                    out=bank[:, t, :],
                    lhsT=w_codes[d][:, t * P : (t + 1) * P].bitcast(FP8X4),
                    lhsT_scale=w_plane[d][:, t * P : (t + 1) * P],
                    rhs=picked_words[e].bitcast(FP8X4),
                    rhs_scale=picked_plane[:, e : e + CH],
                    start=True,
                    stop=True,
                )
            return bank[:].rearrange("p t v -> p v t")

        def by_triple(tile):
            return tile[:].rearrange("p (v t) -> p v t", t=PACK)

        nc.vector.tensor_copy(picked_plane[:], x_plane[:].indirect(offsets[:]))
        picked_early = keep.tile([P, V // 2], U32, name="picked_early", align_bytes=256)
        gather_words(picked_early, [(0, V // 2)])
        round_on_gpsimd(rounded1[:], raw1, 0, slice(0, W1_GPSIMD), every)
        round_on_scalar(rounded1[:], raw1, 0, slice(W1_GPSIMD, P), every)
        quantize_weight(0, 0, rounded1[:])
        picked = keep.tile([P, S - LATE - V // 2], U32, name="picked", tag="raw1", align_bytes=256)
        gather_words(picked, [(V // 2, V), (V, S - LATE)])
        first_bank = [product(0, c, "lo%d" % c) for c in range(NCH)]

        round_on_scalar(low2[:], raw2[0], 0, slice(0, 64), low)
        round_on_gpsimd(high2[:], raw2[0], 0, slice(0, W2_GPSIMD), high)
        round_on_scalar(high2[:], raw2[0], 0, slice(W2_GPSIMD, 64), high)
        round_on_scalar(low2[:], raw2[1], 64, slice(0, 32), low)
        round_on_gpsimd(high2[:], raw2[1], 64, slice(0, 32), high)
        round_on_scalar(low2[:], raw2[2], 96, slice(0, 32), low)
        round_on_scalar(high2[:], raw2[2], 96, slice(0, 32), high)
        first_head = shared.tile([P, 2 * CH * PACK], F32, name="first_head", align_bytes=256, offset=RAW2_AT[0])
        for c in range(2):
            nc.scalar.copy(out=by_triple(first_head)[:, c * CH : (c + 1) * CH], in_=first_bank[c])
        quantize_weight(1, 0, low2[:])
        quantize_weight(1, 2, high2[:])
        picked_late = shared.tile([P, LATE - CH], U32, name="picked_late", align_bytes=256, offset=RAW2_AT[1] + HALF_BYTES // 4)
        gather_words(picked_late, [(S - LATE, S - CH)])
        second_bank = [product(1, c, "hi%d" % c) for c in range(3)]

        round_on_gpsimd(rounded3[:], raw3[0], 0, slice(0, W3_GPSIMD), every)
        round_on_scalar(rounded3[:], raw3[0], 0, slice(W3_GPSIMD, 64), every)
        round_on_gpsimd(rounded3[:], raw3[1], 64, slice(0, 32), every)
        round_on_scalar(rounded3[:], raw3[2], 96, slice(0, 32), every)
        pair0 = keep.tile([P, CH * PACK], F32, name="pair0", align_bytes=256)
        pair1 = keep.tile([P, CH * PACK], F32, name="pair1", align_bytes=256)
        nc.vector.tensor_tensor(by_triple(pair0), second_bank[0], by_triple(first_head)[:, :CH], MULT)
        second_bank.append(product(1, 3, "hi0"))
        nc.vector.tensor_tensor(by_triple(pair1), second_bank[1], by_triple(first_head)[:, CH:], MULT)
        cut = PAIR_VECTOR - 2 * CH
        first_tail = keep.tile([P, 2 * CH * PACK], F32, name="first_tail", align_bytes=256)
        second_tail = keep.tile([P, 2 * CH * PACK], F32, name="second_tail", align_bytes=256)
        nc.scalar.copy(out=by_triple(first_tail)[:, :CH], in_=first_bank[2])
        nc.scalar.copy(out=by_triple(second_tail)[:, cut:CH], in_=second_bank[2][:, cut:])
        nc.scalar.copy(out=by_triple(first_tail)[:, CH:], in_=first_bank[3])
        nc.scalar.copy(out=by_triple(second_tail)[:, CH:], in_=second_bank[3])

        pair_tail = keep.tile([P, 2 * CH * PACK], F32, name="pair_tail", tag="grouped", align_bytes=256)
        quantize_weight(2, 0, rounded3[:, low])
        quantize_weight(2, 2, rounded3[:, high])
        picked_last = keep.tile([P, CH], U32, name="picked_last", tag="raw3384", align_bytes=256)
        gather_words(picked_last, [(S - CH, S)])
        nc.vector.tensor_tensor(by_triple(pair_tail)[:, :cut], second_bank[2][:, :cut], by_triple(first_tail)[:, :cut], MULT)
        for v0, v1 in ((cut, CH), (CH, 2 * CH)):
            cols = slice(v0 * PACK, v1 * PACK)
            nc.gpsimd.tensor_tensor(pair_tail[:, cols], second_tail[:, cols], first_tail[:, cols], MULT)
        pair = [by_triple(pair0), by_triple(pair1), by_triple(pair_tail)[:, :CH], by_triple(pair_tail)[:, CH:]]

        out_v = out.rearrange("(u p) v -> p u v", p=P)
        z = [keep.tile([P, CH, PACK], BF16, name="z%d" % c, align_bytes=256) for c in range(NCH)]
        third_bank = [product(2, c, tag) for c, tag in enumerate(("lo0", "lo1", "hi3", "lo2"))]

        def multiply_third(c, v0, v1):
            nc.vector.tensor_tensor(z[c][:, v0:v1], third_bank[c][:, v0:v1], pair[c][:, v0:v1], MULT)

        def last_product(c, step, banks):
            z_codes = keep.tile([P, CH], U32, name="z_codes%d" % c, align_bytes=256)
            z_plane = keep.tile([P, CH], U8, name="z_plane%d" % c, align_bytes=256)
            for v0 in range(0, CH, step):
                nc.vector.quantize_mx(
                    out=z_codes[:, v0 : v0 + step].bitcast(FP8X4),
                    scales=z_plane[:, v0 : v0 + step],
                    in_=z[c][:, v0 : v0 + step].rearrange("p v t -> p (v t)"),
                )
            for u in range(N // P):
                nc.tensor.matmul_mx(
                    out=banks[u][:, u, :],
                    lhsT=w4_codes[:, 2 * u * P : 2 * (u + 1) * P].bitcast(FP4X4),
                    lhsT_scale=w4_plane[:, u * P : (u + 1) * P],
                    rhs=z_codes[:].bitcast(FP8X4),
                    rhs_scale=z_plane[:],
                    start=True,
                    stop=True,
                )

        def last_layer(c):
            bank = psum.tile([P, PACK, CH], F32, name="bank", tag=("hi1", "hi2", "hi0")[c])
            last_product(c, CH, [bank, bank])
            res = keep.tile([P, N // P, CH], F32, name="res%d" % c, align_bytes=256)
            nc.scalar.activation(res[:], bank[:, 0 : N // P, :], RELU)
            nc.sync.dma_start(out_v[:, :, c * CH : (c + 1) * CH], res[:])

        last = NCH - 1
        for c in range(last):
            multiply_third(c, 0, CH)
        spare = psum.tile([P, PACK * CH], F32, name="bank", tag="lo1")
        nc.tensor.matmul_mx(
            out=spare[:],
            lhsT=w_codes[2][:, :P].bitcast(FP8X4),
            lhsT_scale=w_plane[2][:, :P],
            rhs=w_codes[2][:].bitcast(FP8X4),
            rhs_scale=w_plane[2][:],
            start=True,
            stop=True,
        )
        for c in range(last - 1):
            last_layer(c)
        multiply_third(last, 0, CH // 2)
        last_layer(last - 1)
        multiply_third(last, CH // 2, CH)

        banks = [psum.tile([P, PACK, CH], F32, name="bank", tag=tag) for tag in ("lo3", "lo0")]
        last_product(last, CH // 2, banks)
        res = keep.tile([P, N // P, CH], F32, name="res%d" % last, align_bytes=256)
        nc.vector.tensor_scalar_max(res[:, 0, :], banks[0][:, 0, :], 0.0)
        nc.sync.dma_start(out_v[:, 0, last * CH :], res[:, 0, :])
        nc.scalar.activation(res[:, 1, :], banks[1][:, 1, :], RELU)
        nc.sync.dma_start(out_v[:, 1, last * CH :], res[:, 1, :])
